import numpy as np, ml_dtypes
CORES = [3,11,19,27,35,43,51,59]
N = 8
BF = ml_dtypes.bfloat16
def f(rng, *shape):
    return (rng.standard_normal(shape, dtype=np.float32) * np.exp2(rng.integers(-2, 3, shape[:-1] + (1,)))).astype(BF)
def wide(rng, *shape):
    v = f(rng, *shape).astype(np.float32); k = shape[:-2] + (1, shape[-1])
    return (v * np.exp2(rng.integers(-6, 7, k)) * (rng.random(k) > 0.0625)).astype(BF)
def gentries(a):
    return np.ascontiguousarray(a.reshape(8, 16, -1).transpose(0, 2, 1)).reshape(8, -1)
def gtable(e):
    e = np.asarray(e); return np.ascontiguousarray(e.reshape(8, -1, 16).transpose(0, 2, 1)).reshape(128, -1).astype(np.int32)
R, S, P, CAPP, SM = 2048, 32, 16, 256, 1024
D, W = 2 * S * P, 512 // P
ST = np.arange(D) // (2 * P)
def draws(a, b, cn):
    u = ((a * np.arange(D) + b) >> 2) & 1023
    m = (u * np.sum(cn, 0)[:, ST]) >> 10
    return m, np.sum(m >= np.add.accumulate(cn, 0)[:, :, ST], 0)
def most(own):
    return np.max(np.stack([np.sum(own == q, 1) for q in range(N)]), 0)
def parts(rng, tot, k, hi):
    v = []
    for i in range(k - 1, -1, -1):
        e = int(rng.integers(max(1, tot - i * hi), min(hi, tot - i) + 1)); v.append(e); tot -= e
    return rng.permutation(v)
def latin(rng, al, small):
    cn = np.zeros((N, 8, S), np.int64); turn = (np.arange(N)[:, None] + np.arange(N)) % N
    for g in range(8):
        t = np.concatenate([[1, SM], parts(rng, R - 1 - SM, S // N - 2, SM)]) if small else parts(rng, R, S // N, SM)
        cn[:, g] = np.concatenate([rng.multinomial(e, rng.dirichlet(np.full(N, al)))[turn] for e in t], 1)[:, rng.permutation(S)]
    return cn
def sole(rng):
    cn = np.zeros((N, 8, S), np.int64); q = rng.integers(0, N); k = CAPP // (2 * P)
    for g in range(8):
        n = [k] + [(S - k + i) // (N - 1) for i in range(N - 1)]; o = rng.permutation(np.repeat((q + g + np.arange(N)) % N, n))
        for i in range(N):
            p = np.flatnonzero(o == i); cn[i, g, p] = parts(rng, R, len(p), SM)
    return cn
def even(rng, ends):
    low = rng.choice([0, W - 1], (8, 1)) if ends else rng.integers(0, W, (8, 1))
    return 4 * W * (2 * rng.integers(0, P, (8, 1)) + 1), 4 * (W * rng.integers(0, 2 * P, (8, 1)) + low) + rng.integers(0, 4, (8, 1))
def keys(rng, cn):
    out = []
    for r in range(N):
        a, b = even(rng, False)
        for t in range(4):
            c, e = rng.integers(256, 3841, (8, 1)), rng.integers(0, 4096, (8, 1)); ok = (most(draws(c, e, cn)[1]) <= CAPP)[:, None]
            a, b = np.where(ok, c, a), np.where(ok, e, b)
        out += [a, b]
    return np.concatenate(out, 1)
def make(rng, cn, ab):
    return {"x": f(rng, N, 128, R), "idx": np.stack([gtable(rng.permuted(np.tile(np.arange(R), (8, 1)), axis=1)) for r in range(N)]),
            "counts": cn.astype(np.int32), "ab": np.tile(ab[None], (N, 1, 1)).astype(np.int32)}
def setup_inputs(rng):
    cn = latin(rng, 2.0, False); return make(rng, cn, keys(rng, cn))
def setup_inputs_full(rng):
    ab = rng.integers(0, 4096, (8, 2 * N)); g = rng.integers(0, 8, N); k = 2 * np.arange(N)
    ab[g, k] = 0; ab[(g + 1) % 8, k] = rng.integers(1, 16, N); ab[(g + 2) % 8, k] = 4095; ab[(g + 3) % 8, k] = rng.integers(1024, 3072, N)
    return make(rng, sole(rng), ab)
def setup_inputs_ends(rng):
    d = make(rng, latin(rng, 1.0, False), np.concatenate([e for r in range(N) for e in even(rng, True)], 1))
    d["idx"] = np.stack([gtable(np.where(rng.random((8, 1)) < 0.5, np.arange(R), np.arange(R)[::-1])) for r in range(N)]); return d
def setup_inputs_uneven(rng):
    cn = latin(rng, 0.2, True); return make(rng, cn, keys(rng, cn))
def setup_inputs_spread(rng):
    d = setup_inputs(rng); d["x"] = wide(rng, N, 128, R); return d
def check_inputs(d):
    bad = []; cn = d["counts"].astype(np.int64); ab = d["ab"].astype(np.int64); sz = np.sum(cn, 0)
    if not np.isfinite(d["x"].astype(np.float32)).all(): bad.append("finite")
    if not all((np.sort(gentries(i), 1) == np.arange(R)).all() for i in d["idx"]): bad.append("each_row_once")
    if cn.min() < 0 or (np.sum(cn, 2) != R).any(): bad.append("counts")
    if sz.min() < 1 or sz.max() > SM: bad.append("sizes")
    if ab.min() < 0 or ab.max() > 4095 or (ab != ab[:1]).any(): bad.append("constants")
    if not bad and any(most(draws(ab[0][:, 2 * r:2 * r + 1], ab[0][:, 2 * r + 1:2 * r + 2], cn)[1]).max() > CAPP for r in range(N)): bad.append("cap")
    return bad
def reference(x, idx, counts, ab):
    cn = counts.astype(np.int64); start = np.add.accumulate(cn, 2) - cn; before = np.add.accumulate(cn, 0) - cn
    rows = np.stack([gentries(i) for i in idx]).astype(np.int64); X = x.astype(np.float32).reshape(N, 8, 16, R)
    G = np.arange(8)[:, None]; y = np.zeros((N, 128, S), np.float32)
    for r in range(N):
        c = ab[r].astype(np.int64); m, own = draws(c[:, 2 * r:2 * r + 1], c[:, 2 * r + 1:2 * r + 2], cn)
        row = rows[own, G, start[own, G, ST] + m - before[own, G, ST]]
        v = X[own, G, :, row].reshape(8, S, P, 2, 16)
        z = np.abs(v[:, :, :, 0] - v[:, :, :, 1]); h = P
        while h > 1:
            h >>= 1; z = z[:, :, :h] + z[:, :, h:]
        y[r] = z[:, :, 0].transpose(0, 2, 1).reshape(128, S)
    return {"y": y}

@@ -1,0 +1,299 @@
+from concourse.bass import DstId, RemoteDMATransfer
+from concourse.mybir import AluOpType as A, ActivationFunctionType as F
+
+F32, BF, I32, U16, F16 = "float32", "bfloat16", "int32", "uint16", "float16"
+SCRATCH = {"call": ("dram", [8, 128, 2], I32), "dreq": ("dram", [7, 128, 16], F32)}
+for _dt, _bufs in (
+    (I32, {"abi": [4], "idxi": [128], "nA": [64], "nB": [64], "nC": [64], "n31": [64], "coli": [8], "tI": [64],
+           "uI": [64], "c8": [8, 2, 16], "c64": [32], "pI": [64], "pa": [64], "pb": [64], "pc": [64], "pd": [64],
+           "pe": [64], "pf": [64]}),
+    (F32, {"abf": [4], "tf": [64], "colf": [8], "c1": [4], "win": [2048], "e8": [128], "dI": [16], "uF": [64],
+           "key2": [2, 64], "tw": [2, 16], "t2": [64], "acc": [2, 16], "hs": [2, 8], "k0": [8], "pay": [1024],
+           "req": [128], "va": [4, 128], "dd": [4, 128], "zl": [2, 128], "z1": [2, 128], "z2": [2, 64],
+           "z3": [2, 32], "yt": [32]}),
+    (BF, {"xb": [2048], "xs": [2048], "X": [128], "Gx": [128], "zb": [256], "ident": [128], "i128": [128],
+          "c128": [128], "b4": [128], "nb4": [128], "t4": [128], "ti4": [128], "cmpb": [31, 64], "rank": [64],
+          "sg": [2, 8, 32], "w": [2, 16], "tm": [2, 8, 32], "outb": [7 * 256], "land": [2048]}),
+    (F16, {"blk": [128], "m1": [128], "m2": [128], "m3": [128], "m4": [128], "rr": [16], "um": [1024],
+           "c8f": [2, 128], "c64f": [32], "one": [32], "scn": [32]}),
+    (U16, {"idxu": [128], "offs": [64], "off2": [64], "requ": [128]}),
+):
+    for _n, _s in _bufs.items():
+        SCRATCH[_n] = ("sbuf", [128] + _s, _dt)
+for _b in "ABCDEFGH":
+    SCRATCH["ps" + _b] = ("psum", [128, 512], F32)
+SEMAPHORES = ["qv", "qs", "qt", "qg", "d_c", "d_ab", "d_idx", "d_x", "d_c8", "d_c64", "d_r0", "d_r1", "d_r2",
+              "d_own", "d_y", "cnt_in", "sent", "rq0", "rq1", "rq2", "rows"]
+
+N = 8
+GROUPS = [[1, 2], [3, 4, 5, 6], [7]]
+MAGIC = 12582912.0
+
+
+def rank_program(g, core, T, topo):
+    rank = T.rank_of(core)
+    if rank is None:
+        return
+    S = T.sem
+    Q = {"v": g.vector, "s": g.scalar, "t": g.tensor, "g": g, "y": g.sync}
+    QS = {"v": S.qv, "s": S.qs, "t": S.qt, "g": S.qg}
+    ops = []
+
+    def op(q, fn, deps=(), dma=None):
+        o = {"q": q, "fn": fn, "deps": list(deps), "need": False, "dma": dma}
+        for d in o["deps"]:
+            if isinstance(d, dict):
+                d["need"] = True
+        ops.append(o)
+        return o
+
+    def ts(out, in0, s1, s2, o0, o1=None, deps=()):
+        if o1 is None:
+            return op("v", lambda: g.vector.tensor_scalar(out, in0, s1, None, o0), deps)
+        return op("v", lambda: g.vector.tensor_scalar(out, in0, s1, s2, o0, o1), deps)
+
+    def tt(out, in0, in1, o, deps=()):
+        return op("v", lambda: g.vector.tensor_tensor(out, in0, in1, o), deps)
+
+    def cp(out, in_, deps=()):
+        return op("v", lambda: g.vector.tensor_copy(out, in_), deps)
+
+    def ms(ap, val):
+        return op("v", lambda: g.vector.memset(ap, val))
+
+    def act(out, in_, func, deps=(), **kw):
+        return op("s", lambda: g.scalar.activation(out, in_, func, **kw), deps)
+
+    def mm(out, lhsT, rhs, start, stop, deps=()):
+        return op("t", lambda: g.tensor.matmul(out, lhsT, rhs, start, stop), deps)
+
+    def dma(q, out, in_, sem, deps=()):
+        return op(q, lambda: Q[q].dma_start(out, in_), deps, dma=sem)
+
+    def peer(k):
+        return T.cores[rank ^ k]
+
+    def send(parts, deps):
+        trs = []
+        for k, e0, ne, src, dst, sem in parts:
+            rid, pid, _se = topo.addr(peer(k))
+            m = 0
+            for e in topo.engines(core, peer(k))[e0:e0 + ne]:
+                m |= 1 << e
+            trs.append(RemoteDMATransfer(dst_ids=[DstId(rid=rid, pnc=pid)], dma_engine_mask=m, remote_sem=sem,
+                                         src=src, dst=dst))
+        return op("g", lambda: g.remote_dma_fused(trs, local_sem=S.sent), deps)
+
+    NE = min(len(topo.engines(core, peer(k))) for k in range(1, N))
+
+    dma("y", T.call[rank], T.counts[:], "d_c")
+    dma("s", T.abi[0:8, 0:2], T.ab[:, 2 * rank:2 * rank + 2], "d_ab")
+    dma("s", T.idxi[:], T.idx[:], "d_idx")
+    io_n = op("g", lambda: g.iota(T.nA[:], [[0, 2], [1, 2], [2, 16]], 0, 32))
+    io_g = op("g", lambda: g.iota(T.Gx[:], [[16, 8], [0, 16]], 0, 0, allow_small_or_imprecise_dtypes=True))
+    io_x = op("g", lambda: g.iota(T.X[:], [[1, 128]], 0, 0, allow_small_or_imprecise_dtypes=True))
+    parts = [(k, k - 1, 1 if k < N - 1 else NE - (N - 2), T.call[rank], T.call[rank], S.cnt_in) for k in range(1, N)]
+    send(parts, [("d_c", 16)])
+
+    zb = ms(T.zb[:], 0.0)
+    zw = [act(T.win[:, 256 * j:256 * (j + 1)], T.zb[:], F.Copy, [zb]) for j in range(8)]
+    pre = [ms(T.acc[:, :, 0:1], 32.0), ms(T.acc[:, :, 8:9], -32.0), ms(T.w[:, :, 0:1], 0.0),
+           ms(T.c8f[0:64], 1.0), ms(T.scn[64:128, :], 1.0), ms(T.m2[64:128, :], -0.5 + 2.0 ** -11),
+           ms(T.one[:], 1.0), ms(T.rr[32:64, 0:8], 0.5), ms(T.rr[32:64, 8:9], 0.0)]
+    n0 = T.nA[:, 0:1]
+    sr, an = A.logical_shift_right, A.bitwise_and
+    ci = [ts(T.coli[:, 0:1], n0, 5, None, sr, deps=[io_n]),
+          ts(T.coli[:, 1:2], n0, 5, 112, sr, an),
+          ts(T.coli[:, 2:3], n0, 5, 15, sr, an),
+          ts(T.coli[:, 3:4], n0, 1, 112, sr, an),
+          ts(T.coli[:, 4:5], n0, 8, None, sr)]
+    nb = ts(T.nB[:], T.nA[:], 511, None, an)
+    n31 = ts(T.n31[:], T.nA[:], 31, None, an)
+    cf = cp(T.colf[:, 0:5], T.coli[:, 0:5], [ci[-1]])
+    P, PG, PI, KG, KQ = [T.colf[:, j:j + 1] for j in range(5)]
+    cp(T.nC[:, 0:32], T.nB[:, 0:32], [nb])
+    nc1 = ts(T.nC[:, 32:64], T.nB[:, 32:64], 512.0, None, A.add)
+    tf = ts(T.tf[:], T.n31[:], 1.0 / 32, None, A.mult, deps=[n31])
+    e8 = ts(T.e8[0:8, :], T.Gx[0:8, :], T.colf[0:8, 3:4], None, A.is_equal, deps=[cf, io_g])
+    ts(T.b4[:], T.Gx[:], PG, 0.25, A.is_equal, A.mult)
+    nb4 = ts(T.nb4[:], T.Gx[:], PG, -0.25, A.is_equal, A.mult)
+    blk = ts(T.blk[:], T.Gx[:], PG, None, A.is_equal)
+    c1 = tt(T.c1[:, 0:1], KG, KQ, A.add)
+    dI = ts(T.dI[:], T.X[:, 0:16], PI, None, A.is_equal, deps=[io_x])
+    ident = ts(T.ident[:], T.X[:], P, None, A.is_equal)
+    op("g", lambda: g.affine_select(T.t4[:], T.b4[:], [[1, 128]], A.is_gt, 0.0, 0, -1), [nb4])
+    op("g", lambda: g.affine_select(T.ti4[:], T.nb4[:], [[1, 128]], A.is_ge, 0.0, 0, -1))
+    c128 = op("g", lambda: g.iota(T.c128[:], [[0, 128]], 128, 0, allow_small_or_imprecise_dtypes=True))
+    gconst = op("g", lambda: g.affine_select(T.i128[:], T.c128[:], [[1, 128]], A.is_equal, 0.0, 0, -1), [c128])
+
+    abf = cp(T.abf[0:8, 0:2], T.abi[0:8, 0:2], [("d_ab", 16)])
+    mab = mm(T.psA[:, 0:2], T.e8[0:8, :], T.abf[0:8, 0:2], True, True, [abf, e8])
+    ts(T.m1[0:64, :], T.Gx[0:64, :], T.colf[0:64, 3:4], 1.0 / 1024, A.is_equal, A.mult)
+    ts(T.m4[0:64, :], T.Gx[0:64, :], T.colf[0:64, 3:4], None, A.is_gt)
+    ts(T.m2[0:64, :], T.X[0:64, :], T.c1[0:64, 0:1], None, A.is_equal, deps=[c1])
+    ts(T.m3[0:64, :], T.X[0:64, :], T.c1[0:64, 0:1], -1.0, A.is_ge, A.mult)
+    tI = ts(T.tI[:], T.nC[:], T.psA[:, 0:1], T.psA[:, 1:2], A.mult, A.add, [mab, nc1])
+    ts(T.rr[0:32, 0:8], T.X[0:32, 0:8], T.colf[0:32, 0:1], -1024.0, A.is_gt, A.mult)
+    uI = ts(T.uI[:], T.tI[:], 2, 1023, sr, an, [tI])
+    ts(T.rr[0:32, 8:9], T.colf[0:32, 0:1], 8.0, None, A.is_lt)
+    uF = cp(T.uF[:], T.uI[:], [uI])
+    idxu = cp(T.idxu[:], T.idxi[:], [("d_idx", 16)])
+    tt(T.psB[:, 0:64], T.uF[:], T.tf[:], A.add, [uF, tf])
+    tt(T.key2[:, :, 0:32], T.uF[:], T.tf[:], A.add)
+    key = tt(T.key2[:, :, 32:64], T.uF[:], T.tf[:], A.add)
+    um = [ts(T.um[:, i::16], T.uF[:], T.dI[:, i:i + 1], None, A.mult, deps=[dI]) for i in range(16)]
+    UL = [T.psD, T.psE]
+    ul = [mm(UL[0][:, :], T.blk[:], T.um[:, 0:512], True, True, [um[-1], blk])]
+    for d in range(1, 32):
+        c = tt(T.cmpb[:, d - 1, :], T.psB[:, 0:64], T.key2[:, :, d:d + 32], A.is_gt, [key])
+        rk = mm(T.psC[:, 0:64], T.ident[:], T.cmpb[:, d - 1, :], d == 1, d == 31, [c, ident])
+
+    arrived = [("cnt_in", NE), ("d_c", 16)]
+    dma("y", T.c8[0:8], T.call[:], "d_c8", arrived)
+    dma("s", T.c64[0:64, :], T.call[:], "d_c64", arrived)
+    dma("y", T.xb[:], T.x[:], "d_x", [("d_c8", 16)])
+    rank_c = act(T.rank[:], T.psC[:, 0:64], F.Copy, [rk])
+    TW = [T.psA, T.psB]
+    cv0 = cp(T.c8f[0:8, 0, :], T.c8[0:8, :, 0, :], [("d_c8", 16), pre[-1]])
+    tw0 = mm(TW[0][:, 0:9], T.c8f[0:33, 0, :], T.rr[0:33, 0:9], True, True, [cv0])
+    cv64 = cp(T.c64f[0:64, :], T.c64[0:64, :], [("d_c64", 16)])
+    ctw0 = cp(T.tw[:, 0, 0:9], TW[0][:, 0:9], [tw0])
+    scn = op("v", lambda: g.vector.tensor_tensor_scan(T.scn[0:64, :], T.one[0:64, :], T.c64f[0:64, :], 0.0,
+                                                      A.mult, A.add), [cv64])
+    cv1 = cp(T.c8f[0:8, 1, :], T.c8[0:8, :, 1, :])
+    mm(T.psF[:, 0:32], T.m1[0:64, :], T.c64f[0:64, :], True, True, [cv64])
+    mm(T.psF[:, 32:64], T.m3[0:64, :], T.c64f[0:64, :], True, False)
+    mm(T.psF[:, 32:64], T.m4[0:64, :], T.c64f[0:64, :], False, False)
+    t2m = mm(T.psF[:, 32:64], T.m2[0:65, :], T.scn[0:65, :], False, True, [scn])
+    tw1 = mm(TW[1][:, 0:9], T.c8f[0:33, 1, :], T.rr[0:33, 0:9], True, True, [cv1])
+    ul.append(mm(UL[1][:, :], T.blk[:], T.um[:, 512:1024], True, True))
+    ct2 = cp(T.t2[:], T.psF[:, 0:64], [t2m])
+    ctw1 = cp(T.tw[:, 1, 0:9], TW[1][:, 0:9], [tw1])
+    ctw = [ctw0, ctw1]
+
+    POS = [T.psH, T.psC]
+    PH = [T.psG, T.psF]
+
+    def signs(h):
+        out = []
+        mm(POS[h][:, 0:32], T.ident[:], T.rank[:, 32 * h:32 * h + 32], True, False, [rank_c, gconst])
+        for q in range(1, 8):
+            a = act(T.sg[:, h, q, :], T.uF[:, 32 * h:32 * h + 32], F.Sign, [ctw[h], uF, pre[-1]],
+                    bias=T.tw[:, h, q:q + 1], scale=T.tw[:, h, 8:9], accum_out=T.acc[:, h, q:q + 1])
+            mm(POS[h][:, 0:32], T.i128[:], T.sg[:, h, q, :], False, False, [a])
+            out.append(a)
+        return out
+
+    def pay_v(i):
+        return ts(T.pay[:, i:512:16], UL[0][:, i::16], T.t2[:, i:i + 1], T.t2[:, 32 + i:33 + i], A.mult, A.add,
+                  [ct2, ul[0]])
+
+    def terms(h, dep):
+        for q in range(1, 8):
+            a = act(T.tm[:, h, q, :], T.sg[:, h, q, :], F.Identity, dep,
+                    bias=T.hs[:, h, q:q + 1], scale=T.hs[:, h, q:q + 1])
+            m = mm(POS[h][:, 0:32], T.ident[:], T.tm[:, h, q, :], False, q == 7, [a])
+        return m
+
+    sg0 = signs(0)
+    for i in range(5):
+        pay_v(i)
+    w0 = tt(T.w[:, 0, 1:9], T.acc[:, 0, 0:8], T.acc[:, 0, 1:9], A.subtract, [sg0[-1]])
+    mm(PH[0][:, 0:8], T.t4[:], T.w[:, 0, 1:9], True, False, [w0])
+    ph0 = mm(PH[0][:, 0:8], T.ti4[:], T.w[:, 0, 0:8], False, True)
+    sg1 = signs(1)
+    for i in range(5, 8):
+        pay_v(i)
+    h0 = cp(T.hs[:, 0, :], PH[0][:, 0:8], [ph0])
+    for i in range(8, 16):
+        pv = pay_v(i)
+    pos0 = terms(0, [h0, sg0[-1]])
+    k00 = ts(T.k0[:, 0:1], T.hs[:, 0, 0:1], 2.0, 896.0, A.mult, A.add, [h0])
+    w1 = tt(T.w[:, 1, 1:9], T.acc[:, 1, 0:8], T.acc[:, 1, 1:9], A.subtract, [sg1[-1]])
+    mm(PH[1][:, 0:8], T.t4[:], T.w[:, 1, 1:9], True, False, [w1])
+    mm(PH[1][:, 0:8], T.ti4[:], T.w[:, 1, 0:8], False, False)
+    mm(PH[1][:, 0:8], T.b4[:], T.w[:, 0, 1:9], False, False)
+    ph1 = mm(PH[1][:, 0:8], T.nb4[:], T.w[:, 0, 0:8], False, True)
+    f0 = ts(T.offs[:, 0:32], POS[0][:, 0:32], T.k0[:, 0:1], None, A.add, deps=[pos0, k00])
+    h1 = cp(T.hs[:, 1, :], PH[1][:, 0:8], [ph1])
+    sc0 = cp(T.win[:, :].indirect(T.offs[:, 0:32]), T.pay[:, 0:512], [f0, pv, zw[-1]])
+    for i in range(16):
+        ps = act(T.pay[:, 512 + i:1024:16], UL[1][:, i::16], F.Identity, [ct2, ul[1]],
+                 bias=T.t2[:, 48 + i:49 + i], scale=T.t2[:, 16 + i:17 + i])
+    pos1 = terms(1, [h1, sg1[-1]])
+    k01 = ts(T.k0[:, 4:5], T.hs[:, 1, 0:1], 2.0, 896.0, A.mult, A.add, [h1])
+    f1 = ts(T.offs[:, 32:64], POS[1][:, 0:32], T.k0[:, 4:5], None, A.add, deps=[pos1, k01])
+    sc1 = cp(T.win[:, :].indirect(T.offs[:, 32:64]), T.pay[:, 512:1024], [f1, ps, sc0])
+    xs = act(T.xs[:], T.xb[:, :].indirect(T.idxu[:, :]), F.Copy, [idxu, ("d_x", 16)])
+
+    for n, ks in enumerate(GROUPS):
+        for k in ks:
+            q = rank ^ k
+            dma("y", T.dreq[k - 1], T.win[q::16, 256 * q:256 * (q + 1)], "d_r%d" % n, [sc1])
+    dma("y", T.req[:, 112:128], T.win[rank::16, 256 * rank:256 * (rank + 1)], "d_own")
+    for n, ks in enumerate(GROUPS):
+        ne = NE // len(ks)
+        send([(k, j * ne, ne, T.dreq[k - 1], T.req[:, 16 * (k - 1):16 * k], S["rq%d" % n]) for j, k in enumerate(ks)],
+             [("d_r%d" % n, 16 * len(ks))])
+
+    pI = cp(T.pI[:], T.offs[:], [f1])
+    pa = ts(T.pa[:], T.pI[:], 15, None, an, deps=[pI])
+    ts(T.pb[:], T.pI[:], 4, 15, sr, an)
+    pc = ts(T.pc[:], T.pI[:], 0x700, None, an)
+    pd = ts(T.pd[:], T.pa[:], 16.0, None, A.mult, deps=[pa])
+    pe = tt(T.pe[:], T.pb[:], T.pc[:], A.add, [pc])
+    pf = tt(T.pf[:], T.pd[:], T.pe[:], A.add, [pd, pe])
+    off2 = cp(T.off2[:], T.pf[:], [pf])
+
+    mine = T.land[:, 256 * rank:256 * (rank + 1)]
+    for n, ks in enumerate(GROUPS):
+        lo, hi = ks[0] - 1, ks[-1]
+        last = n == len(GROUPS) - 1
+        top = hi + 1 if last else hi
+        cv = ts(T.requ[:, 16 * lo:16 * top], T.req[:, 16 * lo:16 * top], MAGIC, -MAGIC, A.add, A.add,
+                [("rq%d" % n, NE)] + ([("d_own", 16)] if last else []))
+        mid = hi if last else (lo + hi) // 2
+        gv = cp(T.outb[:, 256 * lo:256 * mid], T.xs[:, :].indirect(T.requ[:, 16 * lo:16 * mid]), [cv, xs])
+        gs = act(mine if last else T.outb[:, 256 * mid:256 * hi],
+                 T.xs[:, :].indirect(T.requ[:, 16 * mid:16 * top]), F.Copy, [cv, xs])
+        ne = NE // len(ks)
+        send([(k, j * ne, ne, T.outb[:, 256 * (k - 1):256 * k], mine, S.rows) for j, k in enumerate(ks)],
+             [gv] if last else [gv, gs])
+    own = gs
+
+    here = [("rows", NE * len(GROUPS)), own, off2]
+    col = [32 * (ch // 2) + 8 * (ch % 2) for ch in range(4)]
+    first = [T.land[:, :].indirect(T.off2[:, c0:c0 + 8]) for c0 in col]
+    va = [cp(T.va[:, 0, :], first[0], here)] + [act(T.va[:, ch, :], first[ch], F.Copy, here) for ch in range(1, 4)]
+    dd = [tt(T.dd[:, ch, :], T.land[:, :].indirect(T.off2[:, col[ch] + 16:col[ch] + 24]), T.va[:, ch, :],
+             A.subtract, [va[ch]]) for ch in range(4)]
+    for h, bank in enumerate((T.psG, T.psH)):
+        act(T.zl[:, h, :], T.dd[:, 2 * h, :], F.Abs, [dd[2 * h]])
+        zu = act(bank[:, 0:128], T.dd[:, 2 * h + 1, :], F.Abs, [dd[2 * h + 1]])
+        z1 = tt(T.z1[:, h, :], T.zl[:, h, :], bank[:, 0:128], A.add, [zu])
+    z2 = tt(T.z2[:], T.z1[:, :, 0:64], T.z1[:, :, 64:128], A.add, [z1])
+    z3 = tt(T.z3[:], T.z2[:, :, 0:32], T.z2[:, :, 32:64], A.add, [z2])
+    z4 = tt(T.yt[:], T.z3[:, :, 0:16], T.z3[:, :, 16:32], A.add, [z3])
+    dma("y", T.y[:], T.yt[:], "d_y", [z4])
+
+    count = {q: 0 for q in QS}
+    seen = {q: {} for q in Q}
+    for o in ops:
+        q = o["q"]
+        want = {}
+        for d in o["deps"]:
+            name, val = ("q" + d["q"], d["at"]) if isinstance(d, dict) else d
+            want[name] = max(want.get(name, 0), val)
+        for name, val in want.items():
+            if seen[q].get(name, 0) < val:
+                Q[q].wait_ge(S[name], val)
+                seen[q][name] = val
+        ins = o["fn"]()
+        if o["dma"] is not None:
+            ins.then_inc(S[o["dma"]], 16)
+        elif o["need"]:
+            count[q] += 1
+            o["at"] = count[q]
+            ins.then_inc(QS[q], 1)
+    g.wait_ge(S.sent, NE * (1 + 2 * len(GROUPS)))
+    g.sync.wait_ge(S.d_y, 16)

@@ -2,32 +2,30 @@ from concourse.bass import DstId, RemoteDMATransfer
 from concourse.mybir import AluOpType as A, ActivationFunctionType as F
 
 F32, BF, I32, U16, F16 = "float32", "bfloat16", "int32", "uint16", "float16"
-SCRATCH = {"call": ("dram", [8, 128, 2], I32), "dreq": ("dram", [7, 128, 16], F32)}
+SCRATCH = {"call": ("dram", [8, 128, 2], I32), "di": ("dram", [8, 128, 16], I32), "li": ("dram", [8, 128, 16], I32),
+           "dx": ("dram", [8, 128, 256], BF), "lx": ("dram", [8, 128, 256], BF),
+           "dz": ("dram", [8, 128, 4], F32), "ly": ("dram", [8, 128, 4], F32)}
 for _dt, _bufs in (
-    (I32, {"abi": [4], "idxi": [128], "nA": [64], "nB": [64], "nC": [64], "n31": [64], "coli": [8], "tI": [64],
-           "uI": [64], "c8": [8, 2, 16], "c64": [32], "pI": [64], "pa": [64], "pb": [64], "pc": [64], "pd": [64],
-           "pe": [64], "pf": [64]}),
-    (F32, {"abf": [4], "tf": [64], "colf": [8], "c1": [4], "win": [2048], "e8": [128], "dI": [16], "uF": [64],
-           "key2": [2, 64], "tw": [2, 16], "t2": [64], "acc": [2, 16], "hs": [2, 8], "k0": [8], "pay": [1024],
-           "req": [128], "va": [4, 128], "dd": [4, 128], "zl": [2, 128], "z1": [2, 128], "z2": [2, 64],
-           "z3": [2, 32], "yt": [32]}),
-    (BF, {"xb": [2048], "xs": [2048], "X": [128], "Gx": [128], "zb": [256], "ident": [128], "i128": [128],
-          "c128": [128], "b4": [128], "nb4": [128], "t4": [128], "ti4": [128], "cmpb": [31, 64], "rank": [64],
-          "sg": [2, 8, 32], "w": [2, 16], "tm": [2, 8, 32], "outb": [7 * 256], "land": [2048]}),
-    (F16, {"blk": [128], "m1": [128], "m2": [128], "m3": [128], "m4": [128], "rr": [16], "um": [1024],
-           "c8f": [2, 128], "c64f": [32], "one": [32], "scn": [32]}),
-    (U16, {"idxu": [128], "offs": [64], "off2": [64], "requ": [128]}),
+    (I32, {"abi": [8], "nA": [32], "nC": [2, 32], "coli": [8], "tI": [2, 4, 32], "uI": [256], "c8": [32],
+           "mI": [256], "idxi": [2, 128]}),
+    (F32, {"abf": [8], "colf": [8], "e2": [128], "uF": [256], "kc": [2, 8], "tb": [2, 8], "ad": [256], "s1": [256],
+           "s2": [256], "zl": [2, 128], "z1": [2, 128], "z2": [2, 64], "z3": [2, 32], "yt": [32]}),
+    (BF, {"x0": [2, 2048], "xs": [4096 + 16], "gt": [4096], "Y": [128], "bp": [176], "bm": [176]}),
+    (F16, {"one": [176], "X": [176], "cpad": [224], "w": [4, 12], "e1": [4], "ev": [12], "sp": [2, 128],
+           "st": [2, 128], "su": [2, 128], "g2": [128]}),
+    (U16, {"idxu": [2, 128], "offs": [256]}),
 ):
     for _n, _s in _bufs.items():
         SCRATCH[_n] = ("sbuf", [128] + _s, _dt)
 for _b in "ABCDEFGH":
     SCRATCH["ps" + _b] = ("psum", [128, 512], F32)
-SEMAPHORES = ["qv", "qs", "qt", "qg", "d_c", "d_ab", "d_idx", "d_x", "d_c8", "d_c64", "d_r0", "d_r1", "d_r2",
-              "d_own", "d_y", "cnt_in", "sent", "rq0", "rq1", "rq2", "rows"]
+SEMAPHORES = ["qv", "qs", "qt", "qg", "d_c", "d_ab", "d_di", "d_oi", "d_dx", "d_ox", "d_c8", "d_i", "d_x0", "d_x1",
+              "d_z", "d_oz", "d_y", "sent", "cnt_in", "idx_in", "a_in", "b0_in", "b1_in", "res_in"]
 
 N = 8
-GROUPS = [[1, 2], [3, 4, 5, 6], [7]]
-MAGIC = 12582912.0
+ZERO = 4096
+BIG = 16384.0
+EPS = 2.0 ** -11
 
 
 def rank_program(g, core, T, topo):
@@ -64,6 +62,11 @@ def rank_program(g, core, T, topo):
     def act(out, in_, func, deps=(), **kw):
         return op("s", lambda: g.scalar.activation(out, in_, func, **kw), deps)
 
+    def gather(q, out, win, offs, deps):
+        if q == "v":
+            return cp(out, win.indirect(offs), deps)
+        return act(out, win.indirect(offs), F.Copy, deps)
+
     def mm(out, lhsT, rhs, start, stop, deps=()):
         return op("t", lambda: g.tensor.matmul(out, lhsT, rhs, start, stop), deps)
 
@@ -73,208 +76,164 @@ def rank_program(g, core, T, topo):
     def peer(k):
         return T.cores[rank ^ k]
 
-    def send(parts, deps):
-        trs = []
-        for k, e0, ne, src, dst, sem in parts:
-            rid, pid, _se = topo.addr(peer(k))
-            m = 0
-            for e in topo.engines(core, peer(k))[e0:e0 + ne]:
-                m |= 1 << e
-            trs.append(RemoteDMATransfer(dst_ids=[DstId(rid=rid, pnc=pid)], dma_engine_mask=m, remote_sem=sem,
-                                         src=src, dst=dst))
-        return op("g", lambda: g.remote_dma_fused(trs, local_sem=S.sent), deps)
-
     NE = min(len(topo.engines(core, peer(k))) for k in range(1, N))
 
+    def send(ks, src, dst, sem, deps):
+        ne = 1
+        while 2 * ne * len(ks) <= NE:
+            ne *= 2
+        trs = []
+        for j, k in enumerate(ks):
+            rid, pid, _se = topo.addr(peer(k))
+            es = topo.engines(core, peer(k))[:NE]
+            m = 0
+            for e in (es[j * ne:(j + 1) * ne] if j < len(ks) - 1 else es[j * ne:]):
+                m |= 1 << e
+            trs.append(RemoteDMATransfer(dst_ids=[DstId(rid=rid, pnc=pid)], dma_engine_mask=m, remote_sem=S[sem],
+                                         src=src(k), dst=dst(k)))
+        return op("g", lambda: g.remote_dma_fused(trs, local_sem=S.sent), deps)
+
+    def slot(k):
+        return 4 * (k & 1) + (rank >> 1)
+
+    everyone = list(range(1, N))
+    mine = slice(16 * rank, 16 * rank + 16)
+
     dma("y", T.call[rank], T.counts[:], "d_c")
-    dma("s", T.abi[0:8, 0:2], T.ab[:, 2 * rank:2 * rank + 2], "d_ab")
-    dma("s", T.idxi[:], T.idx[:], "d_idx")
-    io_n = op("g", lambda: g.iota(T.nA[:], [[0, 2], [1, 2], [2, 16]], 0, 32))
-    io_g = op("g", lambda: g.iota(T.Gx[:], [[16, 8], [0, 16]], 0, 0, allow_small_or_imprecise_dtypes=True))
-    io_x = op("g", lambda: g.iota(T.X[:], [[1, 128]], 0, 0, allow_small_or_imprecise_dtypes=True))
-    parts = [(k, k - 1, 1 if k < N - 1 else NE - (N - 2), T.call[rank], T.call[rank], S.cnt_in) for k in range(1, N)]
-    send(parts, [("d_c", 16)])
+    dma("s", T.abi[0:2, :], T.ab[rank], "d_ab")
+    dma("y", T.di[:], T.idx[:], "d_di")
+    nx = 0
+    for lo, hi in ((0, rank), (rank + 1, N)):
+        if hi > lo:
+            dma("y", T.dx[lo:hi], T.x[16 * lo:16 * hi, :], "d_dx")
+            nx += 16
+    dma("s", T.li[slot(0)], T.idx[mine, :], "d_oi")
+    dma("s", T.lx[slot(0)], T.x[mine, :], "d_ox")
+    io_n = op("g", lambda: g.iota(T.nA[:], [[1, 2], [2, 16]], 0, 32))
+    io_y = op("g", lambda: g.iota(T.Y[:], [[0, 2], [32, 4], [1, 16]], 0, 0, allow_small_or_imprecise_dtypes=True))
+    send(everyone, lambda k: T.call[rank], lambda k: T.call[rank], "cnt_in", [("d_c", 16)])
+    send(everyone, lambda k: T.di[rank ^ k], lambda k: T.li[slot(k)], "idx_in", [("d_di", 16)])
+    for ks, sem in (([2, 4], "a_in"), ([6], "a_in"), ([1, 3], "b0_in"), ([5, 7], "b1_in")):
+        send(ks, lambda k: T.dx[rank ^ k], lambda k: T.lx[slot(k)], sem, [("d_dx", nx)])
 
-    zb = ms(T.zb[:], 0.0)
-    zw = [act(T.win[:, 256 * j:256 * (j + 1)], T.zb[:], F.Copy, [zb]) for j in range(8)]
-    pre = [ms(T.acc[:, :, 0:1], 32.0), ms(T.acc[:, :, 8:9], -32.0), ms(T.w[:, :, 0:1], 0.0),
-           ms(T.c8f[0:64], 1.0), ms(T.scn[64:128, :], 1.0), ms(T.m2[64:128, :], -0.5 + 2.0 ** -11),
-           ms(T.one[:], 1.0), ms(T.rr[32:64, 0:8], 0.5), ms(T.rr[32:64, 8:9], 0.0)]
-    n0 = T.nA[:, 0:1]
+    dma("y", T.c8[0:8, :], T.call[:, mine, :], "d_c8", [("cnt_in", NE), ("d_c", 16)])
+    for blk in range(2):
+        for a in range(2):
+            dma("y", T.idxi[64 * a:64 * a + 64, blk, :], T.li[4 * blk:4 * blk + 4], "d_i",
+                [("idx_in", NE), ("d_oi", 16)])
+    for a in range(2):
+        dma("y", T.x0[64 * a:64 * a + 64, 0, :], T.lx[0:4], "d_x0", [("a_in", 2 * NE), ("d_ox", 16)])
+    for n in range(2):
+        b = ((rank >> 1) & 2) ^ (2 * n)
+        for a in range(2):
+            p0 = 64 * a + 16 * b
+            dma("y", T.x0[p0:p0 + 32, 1, :], T.lx[4 + b:6 + b], "d_x1", [("b%d_in" % n, NE)])
+
     sr, an = A.logical_shift_right, A.bitwise_and
-    ci = [ts(T.coli[:, 0:1], n0, 5, None, sr, deps=[io_n]),
-          ts(T.coli[:, 1:2], n0, 5, 112, sr, an),
-          ts(T.coli[:, 2:3], n0, 5, 15, sr, an),
-          ts(T.coli[:, 3:4], n0, 1, 112, sr, an),
-          ts(T.coli[:, 4:5], n0, 8, None, sr)]
-    nb = ts(T.nB[:], T.nA[:], 511, None, an)
-    n31 = ts(T.n31[:], T.nA[:], 31, None, an)
-    cf = cp(T.colf[:, 0:5], T.coli[:, 0:5], [ci[-1]])
-    P, PG, PI, KG, KQ = [T.colf[:, j:j + 1] for j in range(5)]
-    cp(T.nC[:, 0:32], T.nB[:, 0:32], [nb])
-    nc1 = ts(T.nC[:, 32:64], T.nB[:, 32:64], 512.0, None, A.add)
-    tf = ts(T.tf[:], T.n31[:], 1.0 / 32, None, A.mult, deps=[n31])
-    e8 = ts(T.e8[0:8, :], T.Gx[0:8, :], T.colf[0:8, 3:4], None, A.is_equal, deps=[cf, io_g])
-    ts(T.b4[:], T.Gx[:], PG, 0.25, A.is_equal, A.mult)
-    nb4 = ts(T.nb4[:], T.Gx[:], PG, -0.25, A.is_equal, A.mult)
-    blk = ts(T.blk[:], T.Gx[:], PG, None, A.is_equal)
-    c1 = tt(T.c1[:, 0:1], KG, KQ, A.add)
-    dI = ts(T.dI[:], T.X[:, 0:16], PI, None, A.is_equal, deps=[io_x])
-    ident = ts(T.ident[:], T.X[:], P, None, A.is_equal)
-    op("g", lambda: g.affine_select(T.t4[:], T.b4[:], [[1, 128]], A.is_gt, 0.0, 0, -1), [nb4])
-    op("g", lambda: g.affine_select(T.ti4[:], T.nb4[:], [[1, 128]], A.is_ge, 0.0, 0, -1))
-    c128 = op("g", lambda: g.iota(T.c128[:], [[0, 128]], 128, 0, allow_small_or_imprecise_dtypes=True))
-    gconst = op("g", lambda: g.affine_select(T.i128[:], T.c128[:], [[1, 128]], A.is_equal, 0.0, 0, -1), [c128])
+    one = ms(T.one[:], 1.0)
+    pi0 = 2048.0 * (rank & 1)
+    ms(T.cpad[0:8, 0:96], 0.0)
+    ms(T.cpad[0:8, 128:224], 0.0)
+    ms(T.w[0:8, :, 0:1], 1.0 / 1024)
+    ms(T.w[0:8, :, 6:10], 0.0)
+    n0 = T.nA[:, 0:1]
+    ts(T.coli[:, 0:1], n0, 5, None, sr, deps=[io_n])
+    ts(T.coli[:, 1:2], n0, 1, None, sr)
+    ts(T.coli[:, 2:3], n0, 1, 0x7E0, sr, an)
+    ts(T.coli[:, 3:4], n0, 5, 96, sr, an)
+    ci = ts(T.coli[:, 4:5], n0, 5, 79, sr, an)
+    nc0 = ts(T.nC[:, 0, :], T.nA[:], 511, None, an)
+    xio = op("v", lambda: g.vector.tensor_tensor_scan(T.X[:], T.one[:], T.one[:], -49.0, A.mult, A.add), [one])
+    cf = cp(T.colf[:, 0:5], T.coli[:, 0:5], [ci])
+    nc1 = ts(T.nC[:, 1, :], T.nC[:, 0, :], 512.0, None, A.add, deps=[nc0])
+    P, P32, TC = T.colf[:, 0:1], T.colf[:, 3:4], T.colf[:, 4:5]
+    Q16, Q32 = T.colf[0:8, 1:2], T.colf[0:8, 2:3]
+    e2 = ts(T.e2[0:2, :], T.X[0:2, 48:176], 64.0, T.colf[0:2, 0:1], A.is_ge, A.is_equal, [cf, xio])
+    abf = cp(T.abf[0:2, :], T.abi[0:2, :], [("d_ab", 16)])
+    mab = mm(T.psA[:, 0:8], T.e2[0:2, :], T.abf[0:2, :], True, True, [abf, e2])
+    YB = T.Y[0:8, 0:64:16]
+    ts(T.w[0:8, :, 1], YB, Q16, None, A.is_ge, deps=[io_y])
+    ts(T.w[0:8, :, 3], YB, Q32, 0.5, A.is_equal, A.mult)
+    ts(T.w[0:8, :, 4], YB, Q32, -1.0, A.is_gt, A.mult)
+    ts(T.w[0:8, :, 5], YB, Q16, -1.0, A.is_equal, A.mult)
+    ts(T.w[0:8, :, 10], YB, Q16, None, A.is_equal)
+    e1 = ts(T.e1[0:8, :], YB, 16.0, Q16, A.add, A.is_equal)
+    ts(T.g2[:], T.Y[:], -32.0, P32, A.add, A.is_ge)
+    for h in range(2):
+        ts(T.sp[:, h, :], T.Y[:], 16.0 * h, P, A.add, A.is_equal)
+        su = ts(T.su[:, h, :], T.Y[:], 16.0 * h, P, A.add, A.is_gt)
+    tt(T.w[0:8, :, 2], T.w[0:8, :, 4], T.w[0:8, :, 3], A.subtract, [e1])
+    tt(T.w[0:8, :, 11], T.e1[0:8, :], T.w[0:8, :, 10], A.subtract)
+    for h in range(2):
+        st = tt(T.st[:, h, :], T.su[:, h, :], T.g2[:], A.subtract, [su])
+    for c0, c1, val in ((0, 2, 0.0), (2, 3, EPS), (3, 4, -EPS), (4, 5, pi0), (5, 6, 2048.0 - 2 * pi0)):
+        kc = ms(T.kc[:, :, c0:c1], val)
 
-    abf = cp(T.abf[0:8, 0:2], T.abi[0:8, 0:2], [("d_ab", 16)])
-    mab = mm(T.psA[:, 0:2], T.e8[0:8, :], T.abf[0:8, 0:2], True, True, [abf, e8])
-    ts(T.m1[0:64, :], T.Gx[0:64, :], T.colf[0:64, 3:4], 1.0 / 1024, A.is_equal, A.mult)
-    ts(T.m4[0:64, :], T.Gx[0:64, :], T.colf[0:64, 3:4], None, A.is_gt)
-    ts(T.m2[0:64, :], T.X[0:64, :], T.c1[0:64, 0:1], None, A.is_equal, deps=[c1])
-    ts(T.m3[0:64, :], T.X[0:64, :], T.c1[0:64, 0:1], -1.0, A.is_ge, A.mult)
-    tI = ts(T.tI[:], T.nC[:], T.psA[:, 0:1], T.psA[:, 1:2], A.mult, A.add, [mab, nc1])
-    ts(T.rr[0:32, 0:8], T.X[0:32, 0:8], T.colf[0:32, 0:1], -1024.0, A.is_gt, A.mult)
+    for t in range(4):
+        tI = ts(T.tI[:, :, t, :], T.nC[:], T.psA[:, 2 * t:2 * t + 1], T.psA[:, 2 * t + 1:2 * t + 2], A.mult, A.add,
+                [mab, nc1])
     uI = ts(T.uI[:], T.tI[:], 2, 1023, sr, an, [tI])
-    ts(T.rr[0:32, 8:9], T.colf[0:32, 0:1], 8.0, None, A.is_lt)
     uF = cp(T.uF[:], T.uI[:], [uI])
-    idxu = cp(T.idxu[:], T.idxi[:], [("d_idx", 16)])
-    tt(T.psB[:, 0:64], T.uF[:], T.tf[:], A.add, [uF, tf])
-    tt(T.key2[:, :, 0:32], T.uF[:], T.tf[:], A.add)
-    key = tt(T.key2[:, :, 32:64], T.uF[:], T.tf[:], A.add)
-    um = [ts(T.um[:, i::16], T.uF[:], T.dI[:, i:i + 1], None, A.mult, deps=[dI]) for i in range(16)]
-    UL = [T.psD, T.psE]
-    ul = [mm(UL[0][:, :], T.blk[:], T.um[:, 0:512], True, True, [um[-1], blk])]
-    for d in range(1, 32):
-        c = tt(T.cmpb[:, d - 1, :], T.psB[:, 0:64], T.key2[:, :, d:d + 32], A.is_gt, [key])
-        rk = mm(T.psC[:, 0:64], T.ident[:], T.cmpb[:, d - 1, :], d == 1, d == 31, [c, ident])
 
-    arrived = [("cnt_in", NE), ("d_c", 16)]
-    dma("y", T.c8[0:8], T.call[:], "d_c8", arrived)
-    dma("s", T.c64[0:64, :], T.call[:], "d_c64", arrived)
-    dma("y", T.xb[:], T.x[:], "d_x", [("d_c8", 16)])
-    rank_c = act(T.rank[:], T.psC[:, 0:64], F.Copy, [rk])
-    TW = [T.psA, T.psB]
-    cv0 = cp(T.c8f[0:8, 0, :], T.c8[0:8, :, 0, :], [("d_c8", 16), pre[-1]])
-    tw0 = mm(TW[0][:, 0:9], T.c8f[0:33, 0, :], T.rr[0:33, 0:9], True, True, [cv0])
-    cv64 = cp(T.c64f[0:64, :], T.c64[0:64, :], [("d_c64", 16)])
-    ctw0 = cp(T.tw[:, 0, 0:9], TW[0][:, 0:9], [tw0])
-    scn = op("v", lambda: g.vector.tensor_tensor_scan(T.scn[0:64, :], T.one[0:64, :], T.c64f[0:64, :], 0.0,
-                                                      A.mult, A.add), [cv64])
-    cv1 = cp(T.c8f[0:8, 1, :], T.c8[0:8, :, 1, :])
-    mm(T.psF[:, 0:32], T.m1[0:64, :], T.c64f[0:64, :], True, True, [cv64])
-    mm(T.psF[:, 32:64], T.m3[0:64, :], T.c64f[0:64, :], True, False)
-    mm(T.psF[:, 32:64], T.m4[0:64, :], T.c64f[0:64, :], False, False)
-    t2m = mm(T.psF[:, 32:64], T.m2[0:65, :], T.scn[0:65, :], False, True, [scn])
-    tw1 = mm(TW[1][:, 0:9], T.c8f[0:33, 1, :], T.rr[0:33, 0:9], True, True, [cv1])
-    ul.append(mm(UL[1][:, :], T.blk[:], T.um[:, 512:1024], True, True))
-    ct2 = cp(T.t2[:], T.psF[:, 0:64], [t2m])
-    ctw1 = cp(T.tw[:, 1, 0:9], TW[1][:, 0:9], [tw1])
-    ctw = [ctw0, ctw1]
+    cv = cp(T.cpad[0:8, 96:128], T.c8[0:8, :], [("d_c8", 16)])
+    for b in range(4):
+        m1 = mm(T.psB[:, 0:12], T.cpad[0:8, 96 - 32 * b:224 - 32 * b], T.w[0:8, b, :], b == 0, b == 3, [cv, st])
+    ev = cp(T.ev[:], T.psB[:, 0:12], [m1])
+    for h in range(2):
+        mm(T.psC[:, 6 * h:6 * h + 6], T.sp[:, h, :], T.ev[:, 0:6], True, False, [ev])
+        m2 = mm(T.psC[:, 6 * h:6 * h + 6], T.st[:, h, :], T.ev[:, 6:12], False, True)
+    ts(T.bp[:], T.X[:], TC, None, A.is_equal)
+    tb = tt(T.tb[:, :, 0:6], T.psC[:, 0:12], T.kc[:, :, 0:6], A.add, [m2, kc])
 
-    POS = [T.psH, T.psC]
-    PH = [T.psG, T.psF]
+    offs = []
+    for h in range(2):
+        H = slice(128 * h, 128 * h + 128)
+        H2 = slice(256 + 128 * h, 384 + 128 * h)
+        col = [T.tb[:, h, j:j + 1] for j in range(6)]
+        ad = act(T.ad[:, H], T.uF[:, H], F.Abs, [tb, uF], bias=col[2], scale=col[0])
+        m = ts(T.mI[:, H], T.uF[:, H], col[0], -0.5 + EPS, A.mult, A.add, [tb, uF])
+        pen = ts(T.psD[:, H2], T.ad[:, H], col[3], BIG, A.is_gt, A.mult, [ad])
+        t1 = ts(T.psD[:, H], T.mI[:, H], col[1], col[5], A.is_ge, A.mult, [m])
+        s1 = tt(T.s1[:, H], T.mI[:, H], T.psD[:, H2], A.add, [pen])
+        s2 = tt(T.s2[:, H], T.s1[:, H], T.psD[:, H], A.add, [s1, t1])
+        if h == 0:
+            idxu = cp(T.idxu[:], T.idxi[:], [("d_i", 64)])
+        offs.append(ts(T.offs[:, H], T.s2[:, H], col[4], float(ZERO), A.add, A.min, [s2]))
+    ts(T.bm[:], T.X[:], TC, -1.0, A.is_equal, A.mult)
+    zc = ms(T.xs[:, ZERO:ZERO + 16], 0.0)
 
-    def signs(h):
-        out = []
-        mm(POS[h][:, 0:32], T.ident[:], T.rank[:, 32 * h:32 * h + 32], True, False, [rank_c, gconst])
-        for q in range(1, 8):
-            a = act(T.sg[:, h, q, :], T.uF[:, 32 * h:32 * h + 32], F.Sign, [ctw[h], uF, pre[-1]],
-                    bias=T.tw[:, h, q:q + 1], scale=T.tw[:, h, 8:9], accum_out=T.acc[:, h, q:q + 1])
-            mm(POS[h][:, 0:32], T.i128[:], T.sg[:, h, q, :], False, False, [a])
-            out.append(a)
-        return out
+    done = [zc]
+    for blk, cut, sem in ((0, 80, ("d_x0", 32)), (1, 64, ("d_x1", 64))):
+        for q, c0, c1 in (("s", 0, cut), ("v", cut, 128)):
+            o = 2048 * blk
+            done.append(gather(q, T.xs[:, o + 16 * c0:o + 16 * c1], T.x0[:, blk, :], T.idxu[:, blk, c0:c1],
+                               [idxu, sem]))
 
-    def pay_v(i):
-        return ts(T.pay[:, i:512:16], UL[0][:, i::16], T.t2[:, i:i + 1], T.t2[:, 32 + i:33 + i], A.mult, A.add,
-                  [ct2, ul[0]])
+    ready = [done[-1], done[-2]] + offs
+    last = []
+    for ch in range(8):
+        h, t = divmod(ch, 4)
+        pieces = (("v", 0, 16), ("s", 16, 32)) if ch == 0 else (("v" if ch % 2 else "s", 0, 32),)
+        got = [gather(q, T.gt[:, 512 * ch + 16 * c0:512 * ch + 16 * c1], T.xs[:, :],
+                      T.offs[:, 32 * ch + c0:32 * ch + c1], ready) for q, c0, c1 in pieces]
+        bank = (T.psE, T.psF)[h]
+        view = slice(48 - 16 * t, 176 - 16 * t)
+        mm(bank[:, 0:256], T.bp[:, view], T.gt[:, 512 * ch:512 * ch + 256], t == 0, False, [got[0], zc])
+        m = mm(bank[:, 0:256], T.bm[:, view], T.gt[:, 512 * ch + 256:512 * ch + 512], False, t == 3, [got[-1]])
+        if t == 3:
+            last.append(m)
+    for h, (bank, up) in enumerate(((T.psE, T.psG), (T.psF, T.psH))):
+        act(T.zl[:, h, :], bank[:, 0:128], F.Abs, [last[h]])
+        zu = act(up[:, 0:128], bank[:, 128:256], F.Abs)
+        z1 = tt(T.z1[:, h, :], T.zl[:, h, :], up[:, 0:128], A.add, [zu])
+        z2 = tt(T.z2[:, h, :], T.z1[:, h, 0:64], T.z1[:, h, 64:128], A.add, [z1])
+        z3 = tt(T.z3[:, h, :], T.z2[:, h, 0:32], T.z2[:, h, 32:64], A.add, [z2])
+        z4 = tt(T.yt[:, 16 * h:16 * h + 16], T.z3[:, h, 0:16], T.z3[:, h, 16:32], A.add, [z3])
 
-    def terms(h, dep):
-        for q in range(1, 8):
-            a = act(T.tm[:, h, q, :], T.sg[:, h, q, :], F.Identity, dep,
-                    bias=T.hs[:, h, q:q + 1], scale=T.hs[:, h, q:q + 1])
-            m = mm(POS[h][:, 0:32], T.ident[:], T.tm[:, h, q, :], False, q == 7, [a])
-        return m
-
-    sg0 = signs(0)
-    for i in range(5):
-        pay_v(i)
-    w0 = tt(T.w[:, 0, 1:9], T.acc[:, 0, 0:8], T.acc[:, 0, 1:9], A.subtract, [sg0[-1]])
-    mm(PH[0][:, 0:8], T.t4[:], T.w[:, 0, 1:9], True, False, [w0])
-    ph0 = mm(PH[0][:, 0:8], T.ti4[:], T.w[:, 0, 0:8], False, True)
-    sg1 = signs(1)
-    for i in range(5, 8):
-        pay_v(i)
-    h0 = cp(T.hs[:, 0, :], PH[0][:, 0:8], [ph0])
-    for i in range(8, 16):
-        pv = pay_v(i)
-    pos0 = terms(0, [h0, sg0[-1]])
-    k00 = ts(T.k0[:, 0:1], T.hs[:, 0, 0:1], 2.0, 896.0, A.mult, A.add, [h0])
-    w1 = tt(T.w[:, 1, 1:9], T.acc[:, 1, 0:8], T.acc[:, 1, 1:9], A.subtract, [sg1[-1]])
-    mm(PH[1][:, 0:8], T.t4[:], T.w[:, 1, 1:9], True, False, [w1])
-    mm(PH[1][:, 0:8], T.ti4[:], T.w[:, 1, 0:8], False, False)
-    mm(PH[1][:, 0:8], T.b4[:], T.w[:, 0, 1:9], False, False)
-    ph1 = mm(PH[1][:, 0:8], T.nb4[:], T.w[:, 0, 0:8], False, True)
-    f0 = ts(T.offs[:, 0:32], POS[0][:, 0:32], T.k0[:, 0:1], None, A.add, deps=[pos0, k00])
-    h1 = cp(T.hs[:, 1, :], PH[1][:, 0:8], [ph1])
-    sc0 = cp(T.win[:, :].indirect(T.offs[:, 0:32]), T.pay[:, 0:512], [f0, pv, zw[-1]])
-    for i in range(16):
-        ps = act(T.pay[:, 512 + i:1024:16], UL[1][:, i::16], F.Identity, [ct2, ul[1]],
-                 bias=T.t2[:, 48 + i:49 + i], scale=T.t2[:, 16 + i:17 + i])
-    pos1 = terms(1, [h1, sg1[-1]])
-    k01 = ts(T.k0[:, 4:5], T.hs[:, 1, 0:1], 2.0, 896.0, A.mult, A.add, [h1])
-    f1 = ts(T.offs[:, 32:64], POS[1][:, 0:32], T.k0[:, 4:5], None, A.add, deps=[pos1, k01])
-    sc1 = cp(T.win[:, :].indirect(T.offs[:, 32:64]), T.pay[:, 512:1024], [f1, ps, sc0])
-    xs = act(T.xs[:], T.xb[:, :].indirect(T.idxu[:, :]), F.Copy, [idxu, ("d_x", 16)])
-
-    for n, ks in enumerate(GROUPS):
-        for k in ks:
-            q = rank ^ k
-            dma("y", T.dreq[k - 1], T.win[q::16, 256 * q:256 * (q + 1)], "d_r%d" % n, [sc1])
-    dma("y", T.req[:, 112:128], T.win[rank::16, 256 * rank:256 * (rank + 1)], "d_own")
-    for n, ks in enumerate(GROUPS):
-        ne = NE // len(ks)
-        send([(k, j * ne, ne, T.dreq[k - 1], T.req[:, 16 * (k - 1):16 * k], S["rq%d" % n]) for j, k in enumerate(ks)],
-             [("d_r%d" % n, 16 * len(ks))])
-
-    pI = cp(T.pI[:], T.offs[:], [f1])
-    pa = ts(T.pa[:], T.pI[:], 15, None, an, deps=[pI])
-    ts(T.pb[:], T.pI[:], 4, 15, sr, an)
-    pc = ts(T.pc[:], T.pI[:], 0x700, None, an)
-    pd = ts(T.pd[:], T.pa[:], 16.0, None, A.mult, deps=[pa])
-    pe = tt(T.pe[:], T.pb[:], T.pc[:], A.add, [pc])
-    pf = tt(T.pf[:], T.pd[:], T.pe[:], A.add, [pd, pe])
-    off2 = cp(T.off2[:], T.pf[:], [pf])
-
-    mine = T.land[:, 256 * rank:256 * (rank + 1)]
-    for n, ks in enumerate(GROUPS):
-        lo, hi = ks[0] - 1, ks[-1]
-        last = n == len(GROUPS) - 1
-        top = hi + 1 if last else hi
-        cv = ts(T.requ[:, 16 * lo:16 * top], T.req[:, 16 * lo:16 * top], MAGIC, -MAGIC, A.add, A.add,
-                [("rq%d" % n, NE)] + ([("d_own", 16)] if last else []))
-        mid = hi if last else (lo + hi) // 2
-        gv = cp(T.outb[:, 256 * lo:256 * mid], T.xs[:, :].indirect(T.requ[:, 16 * lo:16 * mid]), [cv, xs])
-        gs = act(mine if last else T.outb[:, 256 * mid:256 * hi],
-                 T.xs[:, :].indirect(T.requ[:, 16 * mid:16 * top]), F.Copy, [cv, xs])
-        ne = NE // len(ks)
-        send([(k, j * ne, ne, T.outb[:, 256 * (k - 1):256 * k], mine, S.rows) for j, k in enumerate(ks)],
-             [gv] if last else [gv, gs])
-    own = gs
-
-    here = [("rows", NE * len(GROUPS)), own, off2]
-    col = [32 * (ch // 2) + 8 * (ch % 2) for ch in range(4)]
-    first = [T.land[:, :].indirect(T.off2[:, c0:c0 + 8]) for c0 in col]
-    va = [cp(T.va[:, 0, :], first[0], here)] + [act(T.va[:, ch, :], first[ch], F.Copy, here) for ch in range(1, 4)]
-    dd = [tt(T.dd[:, ch, :], T.land[:, :].indirect(T.off2[:, col[ch] + 16:col[ch] + 24]), T.va[:, ch, :],
-             A.subtract, [va[ch]]) for ch in range(4)]
-    for h, bank in enumerate((T.psG, T.psH)):
-        act(T.zl[:, h, :], T.dd[:, 2 * h, :], F.Abs, [dd[2 * h]])
-        zu = act(bank[:, 0:128], T.dd[:, 2 * h + 1, :], F.Abs, [dd[2 * h + 1]])
-        z1 = tt(T.z1[:, h, :], T.zl[:, h, :], bank[:, 0:128], A.add, [zu])
-    z2 = tt(T.z2[:], T.z1[:, :, 0:64], T.z1[:, :, 64:128], A.add, [z1])
-    z3 = tt(T.z3[:], T.z2[:, :, 0:32], T.z2[:, :, 32:64], A.add, [z2])
-    z4 = tt(T.yt[:], T.z3[:, :, 0:16], T.z3[:, :, 16:32], A.add, [z3])
-    dma("y", T.y[:], T.yt[:], "d_y", [z4])
+    dma("y", T.dz[:], T.yt[:], "d_z", [z4])
+    dma("s", T.ly[rank], T.yt[mine, :], "d_oz", [z4])
+    send(everyone, lambda k: T.dz[rank ^ k], lambda k: T.ly[rank], "res_in", [("d_z", 16)])
+    dma("y", T.y[:], T.ly[:], "d_y", [("res_in", NE), ("d_oz", 16)])
 
     count = {q: 0 for q in QS}
     seen = {q: {} for q in Q}
@@ -295,5 +254,5 @@ def rank_program(g, core, T, topo):
             count[q] += 1
             o["at"] = count[q]
             ins.then_inc(QS[q], 1)
-    g.wait_ge(S.sent, NE * (1 + 2 * len(GROUPS)))
+    g.wait_ge(S.sent, NE * 7)
     g.sync.wait_ge(S.d_y, 16)

@@ -6,12 +6,12 @@ SCRATCH = {"call": ("dram", [8, 128, 2], I32), "di": ("dram", [8, 128, 16], I32)
            "dx": ("dram", [8, 128, 256], BF), "lx": ("dram", [8, 128, 256], BF),
            "dz": ("dram", [8, 128, 4], F32), "ly": ("dram", [8, 128, 4], F32)}
 for _dt, _bufs in (
-    (I32, {"abi": [8], "nA": [32], "nC": [2, 32], "coli": [8], "tI": [2, 4, 32], "uI": [256], "c8": [32],
-           "mI": [256], "idxi": [2, 128]}),
-    (F32, {"abf": [8], "colf": [8], "e2": [128], "uF": [256], "kc": [2, 8], "tb": [2, 8], "ad": [256], "s1": [256],
-           "s2": [256], "zl": [2, 128], "z1": [2, 128], "z2": [2, 64], "z3": [2, 32], "yt": [32]}),
-    (BF, {"x0": [2, 2048], "xs": [4096 + 16], "gt": [4096], "Y": [128], "bp": [176], "bm": [176]}),
-    (F16, {"one": [176], "X": [176], "cpad": [224], "w": [4, 12], "e1": [4], "ev": [12], "sp": [2, 128],
+    (I32, {"abi": [8], "nA": [32], "nC": [32, 2], "coli": [8], "tI": [32, 4, 2], "uI": [256], "c8": [32],
+           "s2": [256], "idxi": [2, 128]}),
+    (F32, {"abf": [8], "colf": [8], "e2": [128], "uF": [256], "kc": [2, 8], "tb": [2, 8], "ad": [256], "mf": [256],
+           "s1": [256], "zl": [2, 128], "z1": [2, 128], "z2": [2, 64], "z3": [2, 32], "z4": [32], "yt": [32]}),
+    (BF, {"x0": [2, 2048], "xs": [4096 + 16], "gt": [4096], "Y": [128], "bp": [32], "bm": [32]}),
+    (F16, {"one": [128], "X": [128], "cpad": [224], "w": [4, 12], "e1": [4], "ev": [12], "sp": [2, 128],
            "st": [2, 128], "su": [2, 128], "g2": [128]}),
     (U16, {"idxu": [2, 128], "offs": [256]}),
 ):
@@ -19,8 +19,9 @@ for _dt, _bufs in (
         SCRATCH[_n] = ("sbuf", [128] + _s, _dt)
 for _b in "ABCDEFGH":
     SCRATCH["ps" + _b] = ("psum", [128, 512], F32)
-SEMAPHORES = ["qv", "qs", "qt", "qg", "d_c", "d_ab", "d_di", "d_oi", "d_dx", "d_ox", "d_c8", "d_i", "d_x0", "d_x1",
-              "d_z", "d_oz", "d_y", "sent", "cnt_in", "idx_in", "a_in", "b0_in", "b1_in", "res_in"]
+SEMAPHORES = ["qv", "qs", "qt", "qg", "d_c", "d_ab", "d_di", "d_oi", "d_dx", "d_ox", "d_c8", "d_i0", "d_i1", "d_x0",
+              "d_x1", "d_z", "d_oz", "d_y", "sent", "cnt_in", "i0_in", "i1_in", "a_in", "b0_in", "b1_in", "res_in",
+              "h_i", "h_0", "h_1"]
 
 N = 8
 ZERO = 4096
@@ -28,9 +29,48 @@ BIG = 16384.0
 EPS = 2.0 ** -11
 
 
+def helper_of(core, T, topo):
+    for c in topo.cores_of(core):
+        if topo.die(c) != topo.die(core) and all(topo.may_write(c, o) for o in T.cores):
+            return c
+
+
+def shares(engines, n):
+    ne = 1
+    while 2 * ne * n <= len(engines):
+        ne *= 2
+    return [engines[j * ne:(j + 1) * ne] if j < n - 1 else engines[j * ne:] for j in range(n)]
+
+
+def transfer(topo, dst_core, engines, src, dst, sem):
+    rid, pid, _se = topo.addr(dst_core)
+    return RemoteDMATransfer(dst_ids=[DstId(rid=rid, pnc=pid)], dma_engine_mask=sum(1 << e for e in engines),
+                             remote_sem=sem, src=src, dst=dst)
+
+
+def slot(rank, k):
+    return 4 * (k & 1) + (rank >> 1)
+
+
+def helper_program(g, core, rank, T, topo):
+    S = T.sem
+    far = topo.engines(core, T.cores[rank ^ 1])
+    ne = len(far)
+    for wait, ks, src, dst, sems in (("h_i", [1, 3, 5, 7], T.di, T.li, ["i1_in"] * 4),
+                                     ("h_0", [3, 5], T.dx, T.lx, ["b0_in", "b1_in"]),
+                                     ("h_1", [7], T.dx, T.lx, ["b1_in"])):
+        g.wait_ge(S[wait], ne)
+        g.remote_dma_fused([transfer(topo, T.cores[rank ^ k], es, src[rank ^ k], dst[slot(rank, k)], S[sem])
+                            for k, es, sem in zip(ks, shares(far, len(ks)), sems)], local_sem=S.sent)
+    g.wait_ge(S.sent, 3 * ne)
+
+
 def rank_program(g, core, T, topo):
     rank = T.rank_of(core)
     if rank is None:
+        for r, c in enumerate(T.cores):
+            if helper_of(c, T, topo) == core:
+                helper_program(g, core, r, T, topo)
         return
     S = T.sem
     Q = {"v": g.vector, "s": g.scalar, "t": g.tensor, "g": g, "y": g.sync}
@@ -73,28 +113,21 @@ def rank_program(g, core, T, topo):
     def dma(q, out, in_, sem, deps=()):
         return op(q, lambda: Q[q].dma_start(out, in_), deps, dma=sem)
 
-    def peer(k):
-        return T.cores[rank ^ k]
+    helper = helper_of(core, T, topo)
+    far = topo.engines(core, T.cores[rank ^ 1])
+    near = [e for e in topo.engines(core, helper) if e not in far]
+    NE = len(far)
+    sent = [0]
 
-    NE = min(len(topo.engines(core, peer(k))) for k in range(1, N))
-
-    def send(ks, src, dst, sem, deps):
-        ne = 1
-        while 2 * ne * len(ks) <= NE:
-            ne *= 2
-        trs = []
-        for j, k in enumerate(ks):
-            rid, pid, _se = topo.addr(peer(k))
-            es = topo.engines(core, peer(k))[:NE]
-            m = 0
-            for e in (es[j * ne:(j + 1) * ne] if j < len(ks) - 1 else es[j * ne:]):
-                m |= 1 << e
-            trs.append(RemoteDMATransfer(dst_ids=[DstId(rid=rid, pnc=pid)], dma_engine_mask=m, remote_sem=S[sem],
-                                         src=src(k), dst=dst(k)))
+    def send(direct, src, dst, deps, relayed=(), hsem=None):
+        trs = [transfer(topo, T.cores[rank ^ k], es, src(k), dst(k), S[sem])
+               for (k, sem), es in zip(direct, shares(far, len(direct)))]
+        sent[0] += NE
+        if relayed:
+            trs += [transfer(topo, helper, es, src(k), src(k), S[hsem])
+                    for k, es in zip(relayed, shares(near, len(relayed)))]
+            sent[0] += len(near)
         return op("g", lambda: g.remote_dma_fused(trs, local_sem=S.sent), deps)
-
-    def slot(k):
-        return 4 * (k & 1) + (rank >> 1)
 
     everyone = list(range(1, N))
     mine = slice(16 * rank, 16 * rank + 16)
@@ -107,27 +140,29 @@ def rank_program(g, core, T, topo):
         if hi > lo:
             dma("y", T.dx[lo:hi], T.x[16 * lo:16 * hi, :], "d_dx")
             nx += 16
-    dma("s", T.li[slot(0)], T.idx[mine, :], "d_oi")
-    dma("s", T.lx[slot(0)], T.x[mine, :], "d_ox")
-    io_n = op("g", lambda: g.iota(T.nA[:], [[1, 2], [2, 16]], 0, 32))
+    dma("s", T.li[slot(rank, 0)], T.idx[mine, :], "d_oi")
+    dma("s", T.lx[slot(rank, 0)], T.x[mine, :], "d_ox")
+    io_n = op("g", lambda: g.iota(T.nA[:], [[2, 2], [4, 8], [1, 2]], 0, 32))
     io_y = op("g", lambda: g.iota(T.Y[:], [[0, 2], [32, 4], [1, 16]], 0, 0, allow_small_or_imprecise_dtypes=True))
-    send(everyone, lambda k: T.call[rank], lambda k: T.call[rank], "cnt_in", [("d_c", 16)])
-    send(everyone, lambda k: T.di[rank ^ k], lambda k: T.li[slot(k)], "idx_in", [("d_di", 16)])
-    for ks, sem in (([2, 4], "a_in"), ([6], "a_in"), ([1, 3], "b0_in"), ([5, 7], "b1_in")):
-        send(ks, lambda k: T.dx[rank ^ k], lambda k: T.lx[slot(k)], sem, [("d_dx", nx)])
+    send([(k, "cnt_in") for k in everyone], lambda k: T.call[rank], lambda k: T.call[rank], [("d_c", 16)])
+    send([(k, "i0_in") for k in (2, 4, 6)], lambda k: T.di[rank ^ k], lambda k: T.li[slot(rank, k)], [("d_di", 16)],
+         [1, 3, 5, 7], "h_i")
+    for direct, relayed, hsem in (([(2, "a_in"), (4, "a_in")], [3, 5], "h_0"),
+                                  ([(6, "a_in"), (1, "b0_in")], [7], "h_1")):
+        send(direct, lambda k: T.dx[rank ^ k], lambda k: T.lx[slot(rank, k)], [("d_dx", nx)], relayed, hsem)
 
     dma("y", T.c8[0:8, :], T.call[:, mine, :], "d_c8", [("cnt_in", NE), ("d_c", 16)])
-    for blk in range(2):
-        for a in range(2):
-            dma("y", T.idxi[64 * a:64 * a + 64, blk, :], T.li[4 * blk:4 * blk + 4], "d_i",
-                [("idx_in", NE), ("d_oi", 16)])
     for a in range(2):
-        dma("y", T.x0[64 * a:64 * a + 64, 0, :], T.lx[0:4], "d_x0", [("a_in", 2 * NE), ("d_ox", 16)])
-    for n in range(2):
+        dma("y", T.idxi[64 * a:64 * a + 64, 0, :], T.li[0:4], "d_i0", [("i0_in", NE), ("d_oi", 16)])
+    for a in range(2):
+        dma("y", T.x0[64 * a:64 * a + 64, 0, :], T.lx[0:4], "d_x0", [("a_in", 3 * NE // 2), ("d_ox", 16)])
+    for a in range(2):
+        dma("y", T.idxi[64 * a:64 * a + 64, 1, :], T.li[4:8], "d_i1", [("i1_in", NE)])
+    for n, cnt in ((0, NE), (1, 3 * NE // 2)):
         b = ((rank >> 1) & 2) ^ (2 * n)
         for a in range(2):
             p0 = 64 * a + 16 * b
-            dma("y", T.x0[p0:p0 + 32, 1, :], T.lx[4 + b:6 + b], "d_x1", [("b%d_in" % n, NE)])
+            dma("y", T.x0[p0:p0 + 32, 1, :], T.lx[4 + b:6 + b], "d_x1", [("b%d_in" % n, cnt)])
 
     sr, an = A.logical_shift_right, A.bitwise_and
     one = ms(T.one[:], 1.0)
@@ -135,28 +170,33 @@ def rank_program(g, core, T, topo):
     ms(T.cpad[0:8, 0:96], 0.0)
     ms(T.cpad[0:8, 128:224], 0.0)
     ms(T.w[0:8, :, 0:1], 1.0 / 1024)
-    ms(T.w[0:8, :, 6:10], 0.0)
+    ms(T.w[0:8, :, 6:7], 0.0)
+    ms(T.w[0:8, :, 8:10], 0.0)
+    xio = op("v", lambda: g.vector.tensor_tensor_scan(T.X[:], T.one[:], T.one[:], -1.0, A.mult, A.add), [one])
+    for c0, c1, val in ((0, 1, 0.0), (1, 2, pi0 - 0.5), (2, 3, EPS), (3, 4, -EPS), (4, 5, pi0 - 0.5 + EPS),
+                        (5, 6, 2048.0 - 2 * pi0)):
+        kc = ms(T.kc[:, :, c0:c1], val)
     n0 = T.nA[:, 0:1]
     ts(T.coli[:, 0:1], n0, 5, None, sr, deps=[io_n])
     ts(T.coli[:, 1:2], n0, 1, None, sr)
     ts(T.coli[:, 2:3], n0, 1, 0x7E0, sr, an)
     ts(T.coli[:, 3:4], n0, 5, 96, sr, an)
-    ci = ts(T.coli[:, 4:5], n0, 5, 79, sr, an)
-    nc0 = ts(T.nC[:, 0, :], T.nA[:], 511, None, an)
-    xio = op("v", lambda: g.vector.tensor_tensor_scan(T.X[:], T.one[:], T.one[:], -49.0, A.mult, A.add), [one])
-    cf = cp(T.colf[:, 0:5], T.coli[:, 0:5], [ci])
-    nc1 = ts(T.nC[:, 1, :], T.nC[:, 0, :], 512.0, None, A.add, deps=[nc0])
-    P, P32, TC = T.colf[:, 0:1], T.colf[:, 3:4], T.colf[:, 4:5]
+    ts(T.coli[:, 4:5], n0, 7, 16, sr, an)
+    ci = ts(T.coli[:, 5:6], n0, 5, 15, sr, an)
+    nc0 = ts(T.nC[:, :, 0], T.nA[:], 511, None, an)
+    cf = cp(T.colf[:, 0:6], T.coli[:, 0:6], [ci])
+    nc1 = ts(T.nC[:, :, 1], T.nC[:, :, 0], 512.0, None, A.add, deps=[nc0])
+    P, P32 = T.colf[:, 0:1], T.colf[:, 3:4]
     Q16, Q32 = T.colf[0:8, 1:2], T.colf[0:8, 2:3]
-    e2 = ts(T.e2[0:2, :], T.X[0:2, 48:176], 64.0, T.colf[0:2, 0:1], A.is_ge, A.is_equal, [cf, xio])
+    e2 = ts(T.e2[0:2, :], T.X[0:2, :], 64.0, T.colf[0:2, 0:1], A.is_ge, A.is_equal, [cf, xio])
     abf = cp(T.abf[0:2, :], T.abi[0:2, :], [("d_ab", 16)])
     mab = mm(T.psA[:, 0:8], T.e2[0:2, :], T.abf[0:2, :], True, True, [abf, e2])
     YB = T.Y[0:8, 0:64:16]
-    ts(T.w[0:8, :, 1], YB, Q16, None, A.is_ge, deps=[io_y])
+    for j in (1, 7, 10):
+        ts(T.w[0:8, :, j], YB, Q16, None, A.is_equal, deps=[io_y])
     ts(T.w[0:8, :, 3], YB, Q32, 0.5, A.is_equal, A.mult)
     ts(T.w[0:8, :, 4], YB, Q32, -1.0, A.is_gt, A.mult)
     ts(T.w[0:8, :, 5], YB, Q16, -1.0, A.is_equal, A.mult)
-    ts(T.w[0:8, :, 10], YB, Q16, None, A.is_equal)
     e1 = ts(T.e1[0:8, :], YB, 16.0, Q16, A.add, A.is_equal)
     ts(T.g2[:], T.Y[:], -32.0, P32, A.add, A.is_ge)
     for h in range(2):
@@ -166,8 +206,6 @@ def rank_program(g, core, T, topo):
     tt(T.w[0:8, :, 11], T.e1[0:8, :], T.w[0:8, :, 10], A.subtract)
     for h in range(2):
         st = tt(T.st[:, h, :], T.su[:, h, :], T.g2[:], A.subtract, [su])
-    for c0, c1, val in ((0, 2, 0.0), (2, 3, EPS), (3, 4, -EPS), (4, 5, pi0), (5, 6, 2048.0 - 2 * pi0)):
-        kc = ms(T.kc[:, :, c0:c1], val)
 
     for t in range(4):
         tI = ts(T.tI[:, :, t, :], T.nC[:], T.psA[:, 2 * t:2 * t + 1], T.psA[:, 2 * t + 1:2 * t + 2], A.mult, A.add,
@@ -178,49 +216,46 @@ def rank_program(g, core, T, topo):
     cv = cp(T.cpad[0:8, 96:128], T.c8[0:8, :], [("d_c8", 16)])
     for b in range(4):
         m1 = mm(T.psB[:, 0:12], T.cpad[0:8, 96 - 32 * b:224 - 32 * b], T.w[0:8, b, :], b == 0, b == 3, [cv, st])
+    bp = ts(T.bp[:], T.X[:, 0:32], T.colf[:, 4:5], T.colf[:, 5:6], A.subtract, A.is_equal)
     ev = cp(T.ev[:], T.psB[:, 0:12], [m1])
+    bm = ts(T.bm[:], T.bp[:], -1.0, None, A.mult, deps=[bp])
     for h in range(2):
         mm(T.psC[:, 6 * h:6 * h + 6], T.sp[:, h, :], T.ev[:, 0:6], True, False, [ev])
         m2 = mm(T.psC[:, 6 * h:6 * h + 6], T.st[:, h, :], T.ev[:, 6:12], False, True)
-    ts(T.bp[:], T.X[:], TC, None, A.is_equal)
-    tb = tt(T.tb[:, :, 0:6], T.psC[:, 0:12], T.kc[:, :, 0:6], A.add, [m2, kc])
-
-    offs = []
-    for h in range(2):
-        H = slice(128 * h, 128 * h + 128)
-        H2 = slice(256 + 128 * h, 384 + 128 * h)
-        col = [T.tb[:, h, j:j + 1] for j in range(6)]
-        ad = act(T.ad[:, H], T.uF[:, H], F.Abs, [tb, uF], bias=col[2], scale=col[0])
-        m = ts(T.mI[:, H], T.uF[:, H], col[0], -0.5 + EPS, A.mult, A.add, [tb, uF])
-        pen = ts(T.psD[:, H2], T.ad[:, H], col[3], BIG, A.is_gt, A.mult, [ad])
-        t1 = ts(T.psD[:, H], T.mI[:, H], col[1], col[5], A.is_ge, A.mult, [m])
-        s1 = tt(T.s1[:, H], T.mI[:, H], T.psD[:, H2], A.add, [pen])
-        s2 = tt(T.s2[:, H], T.s1[:, H], T.psD[:, H], A.add, [s1, t1])
-        if h == 0:
-            idxu = cp(T.idxu[:], T.idxi[:], [("d_i", 64)])
-        offs.append(ts(T.offs[:, H], T.s2[:, H], col[4], float(ZERO), A.add, A.min, [s2]))
-    ts(T.bm[:], T.X[:], TC, -1.0, A.is_equal, A.mult)
     zc = ms(T.xs[:, ZERO:ZERO + 16], 0.0)
+    tb = tt(T.tb[:, :, 0:6], T.psC[:, 0:12], T.kc[:, :, 0:6], A.add, [m2, kc])
+    idxu = [cp(T.idxu[:, 0, :], T.idxi[:, 0, :], [("d_i0", 32)])]
 
-    done = [zc]
+    for h in range(2):
+        col = [T.tb[:, h, j:j + 1] for j in range(6)]
+        mf = act(T.mf[:, h::2], T.uF[:, h::2], F.Identity, [tb, uF], bias=col[4], scale=col[0])
+        ad = act(T.ad[:, h::2], T.uF[:, h::2], F.Abs, bias=col[2], scale=col[0])
+        ts(T.psD[:, h:256:2], T.mf[:, h::2], col[1], col[5], A.is_ge, A.mult, [mf, tb])
+        pen = ts(T.psD[:, 256 + h::2], T.ad[:, h::2], col[3], BIG, A.is_gt, A.mult, [ad])
+    s1 = tt(T.s1[:], T.mf[:], T.psD[:, 0:256], A.add, [pen])
+    s2 = tt(T.s2[:], T.s1[:], T.psD[:, 256:512], A.add, [s1])
+    offs = ts(T.offs[:], T.s2[:], float(ZERO), None, A.min, deps=[s2])
+
+    done = []
     for blk, cut, sem in ((0, 80, ("d_x0", 32)), (1, 64, ("d_x1", 64))):
+        if blk == 1:
+            idxu.append(cp(T.idxu[:, 1, :], T.idxi[:, 1, :], [("d_i1", 32)]))
         for q, c0, c1 in (("s", 0, cut), ("v", cut, 128)):
             o = 2048 * blk
             done.append(gather(q, T.xs[:, o + 16 * c0:o + 16 * c1], T.x0[:, blk, :], T.idxu[:, blk, c0:c1],
-                               [idxu, sem]))
+                               [idxu[blk], sem]))
 
-    ready = [done[-1], done[-2]] + offs
+    ready = [done[-1], done[-2], offs]
+    z3 = []
     last = []
     for ch in range(8):
-        h, t = divmod(ch, 4)
-        pieces = (("v", 0, 16), ("s", 16, 32)) if ch == 0 else (("v" if ch % 2 else "s", 0, 32),)
-        got = [gather(q, T.gt[:, 512 * ch + 16 * c0:512 * ch + 16 * c1], T.xs[:, :],
-                      T.offs[:, 32 * ch + c0:32 * ch + c1], ready) for q, c0, c1 in pieces]
-        bank = (T.psE, T.psF)[h]
-        view = slice(48 - 16 * t, 176 - 16 * t)
-        mm(bank[:, 0:256], T.bp[:, view], T.gt[:, 512 * ch:512 * ch + 256], t == 0, False, [got[0], zc])
-        m = mm(bank[:, 0:256], T.bm[:, view], T.gt[:, 512 * ch + 256:512 * ch + 512], False, t == 3, [got[-1]])
-        if t == 3:
+        got = gather("vs"[ch % 2], T.gt[:, 512 * ch:512 * ch + 512], T.xs[:, :], T.offs[:, 32 * ch:32 * ch + 32], ready)
+        bank = (T.psE, T.psF)[ch // 4]
+        for j in range(2 * ch, 2 * ch + 2):
+            out = bank[:, 32 * (j % 8):32 * (j % 8) + 32]
+            mm(out, T.gt[:, 256 * j:256 * j + 128], T.bp[:], True, False, [got, bm])
+            m = mm(out, T.gt[:, 256 * j + 128:256 * j + 256], T.bm[:], False, True)
+        if ch % 4 == 3:
             last.append(m)
     for h, (bank, up) in enumerate(((T.psE, T.psG), (T.psF, T.psH))):
         act(T.zl[:, h, :], bank[:, 0:128], F.Abs, [last[h]])
@@ -228,11 +263,15 @@ def rank_program(g, core, T, topo):
         z1 = tt(T.z1[:, h, :], T.zl[:, h, :], up[:, 0:128], A.add, [zu])
         z2 = tt(T.z2[:, h, :], T.z1[:, h, 0:64], T.z1[:, h, 64:128], A.add, [z1])
         z3 = tt(T.z3[:, h, :], T.z2[:, h, 0:32], T.z2[:, h, 32:64], A.add, [z2])
-        z4 = tt(T.yt[:, 16 * h:16 * h + 16], T.z3[:, h, 0:16], T.z3[:, h, 16:32], A.add, [z3])
+    z4 = tt(T.z4[:], T.z3[:, 0, :], T.z3[:, 1, :], A.add, [z3])
+    yt = op("v", lambda: g.vector.transpose(T.yt[:], T.z4[:]), [z4])
 
-    dma("y", T.dz[:], T.yt[:], "d_z", [z4])
-    dma("s", T.ly[rank], T.yt[mine, :], "d_oz", [z4])
-    send(everyone, lambda k: T.dz[rank ^ k], lambda k: T.ly[rank], "res_in", [("d_z", 16)])
+    def place(r):
+        return 2 * (r % 4) + r // 4
+
+    dma("y", T.dz[:], T.yt[:], "d_z", [yt])
+    dma("s", T.ly[rank], T.yt[16 * place(rank):16 * place(rank) + 16, :], "d_oz", [yt])
+    send([(k, "res_in") for k in everyone], lambda k: T.dz[place(rank ^ k)], lambda k: T.ly[rank], [("d_z", 16)])
     dma("y", T.y[:], T.ly[:], "d_y", [("res_in", NE), ("d_oz", 16)])
 
     count = {q: 0 for q in QS}
@@ -254,5 +293,5 @@ def rank_program(g, core, T, topo):
             count[q] += 1
             o["at"] = count[q]
             ins.then_inc(QS[q], 1)
-    g.wait_ge(S.sent, NE * 7)
+    g.wait_ge(S.sent, sent[0])
     g.sync.wait_ge(S.d_y, 16)

from concourse.bass import DstId, RemoteDMATransfer
from concourse.mybir import AluOpType as A, ActivationFunctionType as F

F32, BF, I32, U16, F16 = "float32", "bfloat16", "int32", "uint16", "float16"
SCRATCH = {"call": ("dram", [8, 128, 2], I32), "di": ("dram", [8, 128, 16], I32), "li": ("dram", [8, 128, 16], I32),
           "dx": ("dram", [8, 128, 256], BF), "lx": ("dram", [8, 128, 256], BF),
           "dz": ("dram", [8, 128, 4], F32), "ly": ("dram", [8, 128, 4], F32)}
for _dt, _bufs in (
    (I32, {"abi": [8], "nA": [32], "nC": [32, 2], "coli": [8], "tI": [32, 4, 2], "uI": [256], "c8": [32],
           "s2": [256], "idxi": [2, 128]}),
    (F32, {"abf": [8], "colf": [8], "e2": [128], "uF": [256], "kc": [2, 8], "tb": [2, 8], "ad": [256], "mf": [256],
           "s1": [256], "zl": [2, 128], "z1": [2, 128], "z2": [2, 64], "z3": [2, 32], "z4": [32], "yt": [32]}),
    (BF, {"x0": [2, 2048], "xs": [4096 + 16], "gt": [4096], "Y": [128], "bp": [32], "bm": [32]}),
    (F16, {"one": [128], "X": [128], "cpad": [224], "w": [4, 12], "e1": [4], "ev": [12], "sp": [2, 128],
           "st": [2, 128], "su": [2, 128], "g2": [128]}),
    (U16, {"idxu": [2, 128], "offs": [256]}),
):
    for _n, _s in _bufs.items():
        SCRATCH[_n] = ("sbuf", [128] + _s, _dt)
for _b in "ABCDEFGH":
    SCRATCH["ps" + _b] = ("psum", [128, 512], F32)
SEMAPHORES = ["qv", "qs", "qt", "qg", "d_c", "d_ab", "d_di", "d_oi", "d_dx", "d_ox", "d_c8", "d_i0", "d_i1", "d_x0",
              "d_x1", "d_z", "d_oz", "d_y", "sent", "cnt_in", "i0_in", "i1_in", "a_in", "b0_in", "b1_in", "res_in",
              "h_i", "h_0", "h_1"]

N = 8
ZERO = 4096
BIG = 16384.0
EPS = 2.0 ** -11


def helper_of(core, T, topo):
    for c in topo.cores_of(core):
        if topo.die(c) != topo.die(core) and all(topo.may_write(c, o) for o in T.cores):
            return c


def shares(engines, n):
    ne = 1
    while 2 * ne * n <= len(engines):
        ne *= 2
    return [engines[j * ne:(j + 1) * ne] if j < n - 1 else engines[j * ne:] for j in range(n)]


def transfer(topo, dst_core, engines, src, dst, sem):
    rid, pid, _se = topo.addr(dst_core)
    return RemoteDMATransfer(dst_ids=[DstId(rid=rid, pnc=pid)], dma_engine_mask=sum(1 << e for e in engines),
                             remote_sem=sem, src=src, dst=dst)


def slot(rank, k):
    return 4 * (k & 1) + (rank >> 1)


def helper_program(g, core, rank, T, topo):
    S = T.sem
    far = topo.engines(core, T.cores[rank ^ 1])
    ne = len(far)
    for wait, ks, src, dst, sems in (("h_i", [1, 3, 5, 7], T.di, T.li, ["i1_in"] * 4),
                                     ("h_0", [3, 5], T.dx, T.lx, ["b0_in", "b1_in"]),
                                     ("h_1", [7], T.dx, T.lx, ["b1_in"])):
        g.wait_ge(S[wait], ne)
        g.remote_dma_fused([transfer(topo, T.cores[rank ^ k], es, src[rank ^ k], dst[slot(rank, k)], S[sem])
                            for k, es, sem in zip(ks, shares(far, len(ks)), sems)], local_sem=S.sent)
    g.wait_ge(S.sent, 3 * ne)


def rank_program(g, core, T, topo):
    rank = T.rank_of(core)
    if rank is None:
        for r, c in enumerate(T.cores):
            if helper_of(c, T, topo) == core:
                helper_program(g, core, r, T, topo)
        return
    S = T.sem
    Q = {"v": g.vector, "s": g.scalar, "t": g.tensor, "g": g, "y": g.sync}
    QS = {"v": S.qv, "s": S.qs, "t": S.qt, "g": S.qg}
    ops = []

    def op(q, fn, deps=(), dma=None):
        o = {"q": q, "fn": fn, "deps": list(deps), "need": False, "dma": dma}
        for d in o["deps"]:
            if isinstance(d, dict):
                d["need"] = True
        ops.append(o)
        return o

    def ts(out, in0, s1, s2, o0, o1=None, deps=()):
        if o1 is None:
            return op("v", lambda: g.vector.tensor_scalar(out, in0, s1, None, o0), deps)
        return op("v", lambda: g.vector.tensor_scalar(out, in0, s1, s2, o0, o1), deps)

    def tt(out, in0, in1, o, deps=()):
        return op("v", lambda: g.vector.tensor_tensor(out, in0, in1, o), deps)

    def cp(out, in_, deps=()):
        return op("v", lambda: g.vector.tensor_copy(out, in_), deps)

    def ms(ap, val):
        return op("v", lambda: g.vector.memset(ap, val))

    def act(out, in_, func, deps=(), **kw):
        return op("s", lambda: g.scalar.activation(out, in_, func, **kw), deps)

    def gather(q, out, win, offs, deps):
        if q == "v":
            return cp(out, win.indirect(offs), deps)
        return act(out, win.indirect(offs), F.Copy, deps)

    def mm(out, lhsT, rhs, start, stop, deps=()):
        return op("t", lambda: g.tensor.matmul(out, lhsT, rhs, start, stop), deps)

    def dma(q, out, in_, sem, deps=()):
        return op(q, lambda: Q[q].dma_start(out, in_), deps, dma=sem)

    helper = helper_of(core, T, topo)
    far = topo.engines(core, T.cores[rank ^ 1])
    near = [e for e in topo.engines(core, helper) if e not in far]
    NE = len(far)
    sent = [0]

    def send(direct, src, dst, deps, relayed=(), hsem=None):
        trs = [transfer(topo, T.cores[rank ^ k], es, src(k), dst(k), S[sem])
               for (k, sem), es in zip(direct, shares(far, len(direct)))]
        sent[0] += NE
        if relayed:
            trs += [transfer(topo, helper, es, src(k), src(k), S[hsem])
                    for k, es in zip(relayed, shares(near, len(relayed)))]
            sent[0] += len(near)
        return op("g", lambda: g.remote_dma_fused(trs, local_sem=S.sent), deps)

    everyone = list(range(1, N))
    mine = slice(16 * rank, 16 * rank + 16)

    dma("y", T.call[rank], T.counts[:], "d_c")
    dma("s", T.abi[0:2, :], T.ab[rank], "d_ab")
    dma("y", T.di[:], T.idx[:], "d_di")
    nx = 0
    for lo, hi in ((0, rank), (rank + 1, N)):
        if hi > lo:
            dma("y", T.dx[lo:hi], T.x[16 * lo:16 * hi, :], "d_dx")
            nx += 16
    dma("s", T.li[slot(rank, 0)], T.idx[mine, :], "d_oi")
    dma("s", T.lx[slot(rank, 0)], T.x[mine, :], "d_ox")
    io_n = op("g", lambda: g.iota(T.nA[:], [[2, 2], [4, 8], [1, 2]], 0, 32))
    io_y = op("g", lambda: g.iota(T.Y[:], [[0, 2], [32, 4], [1, 16]], 0, 0, allow_small_or_imprecise_dtypes=True))
    send([(k, "cnt_in") for k in everyone], lambda k: T.call[rank], lambda k: T.call[rank], [("d_c", 16)])
    send([(k, "i0_in") for k in (2, 4, 6)], lambda k: T.di[rank ^ k], lambda k: T.li[slot(rank, k)], [("d_di", 16)],
         [1, 3, 5, 7], "h_i")
    for direct, relayed, hsem in (([(2, "a_in"), (4, "a_in")], [3, 5], "h_0"),
                                  ([(6, "a_in"), (1, "b0_in")], [7], "h_1")):
        send(direct, lambda k: T.dx[rank ^ k], lambda k: T.lx[slot(rank, k)], [("d_dx", nx)], relayed, hsem)

    dma("y", T.c8[0:8, :], T.call[:, mine, :], "d_c8", [("cnt_in", NE), ("d_c", 16)])
    for a in range(2):
        dma("y", T.idxi[64 * a:64 * a + 64, 0, :], T.li[0:4], "d_i0", [("i0_in", NE), ("d_oi", 16)])
    for a in range(2):
        dma("y", T.x0[64 * a:64 * a + 64, 0, :], T.lx[0:4], "d_x0", [("a_in", 3 * NE // 2), ("d_ox", 16)])
    for a in range(2):
        dma("y", T.idxi[64 * a:64 * a + 64, 1, :], T.li[4:8], "d_i1", [("i1_in", NE)])
    for n, cnt in ((0, NE), (1, 3 * NE // 2)):
        b = ((rank >> 1) & 2) ^ (2 * n)
        for a in range(2):
            p0 = 64 * a + 16 * b
            dma("y", T.x0[p0:p0 + 32, 1, :], T.lx[4 + b:6 + b], "d_x1", [("b%d_in" % n, cnt)])

    sr, an = A.logical_shift_right, A.bitwise_and
    one = ms(T.one[:], 1.0)
    pi0 = 2048.0 * (rank & 1)
    ms(T.cpad[0:8, 0:96], 0.0)
    ms(T.cpad[0:8, 128:224], 0.0)
    ms(T.w[0:8, :, 0:1], 1.0 / 1024)
    ms(T.w[0:8, :, 6:7], 0.0)
    ms(T.w[0:8, :, 8:10], 0.0)
    xio = op("v", lambda: g.vector.tensor_tensor_scan(T.X[:], T.one[:], T.one[:], -1.0, A.mult, A.add), [one])
    for c0, c1, val in ((0, 1, 0.0), (1, 2, pi0 - 0.5), (2, 3, EPS), (3, 4, -EPS), (4, 5, pi0 - 0.5 + EPS),
                        (5, 6, 2048.0 - 2 * pi0)):
        kc = ms(T.kc[:, :, c0:c1], val)
    n0 = T.nA[:, 0:1]
    ts(T.coli[:, 0:1], n0, 5, None, sr, deps=[io_n])
    ts(T.coli[:, 1:2], n0, 1, None, sr)
    ts(T.coli[:, 2:3], n0, 1, 0x7E0, sr, an)
    ts(T.coli[:, 3:4], n0, 5, 96, sr, an)
    ts(T.coli[:, 4:5], n0, 7, 16, sr, an)
    ci = ts(T.coli[:, 5:6], n0, 5, 15, sr, an)
    nc0 = ts(T.nC[:, :, 0], T.nA[:], 511, None, an)
    cf = cp(T.colf[:, 0:6], T.coli[:, 0:6], [ci])
    nc1 = ts(T.nC[:, :, 1], T.nC[:, :, 0], 512.0, None, A.add, deps=[nc0])
    P, P32 = T.colf[:, 0:1], T.colf[:, 3:4]
    Q16, Q32 = T.colf[0:8, 1:2], T.colf[0:8, 2:3]
    e2 = ts(T.e2[0:2, :], T.X[0:2, :], 64.0, T.colf[0:2, 0:1], A.is_ge, A.is_equal, [cf, xio])
    abf = cp(T.abf[0:2, :], T.abi[0:2, :], [("d_ab", 16)])
    mab = mm(T.psA[:, 0:8], T.e2[0:2, :], T.abf[0:2, :], True, True, [abf, e2])
    YB = T.Y[0:8, 0:64:16]
    for j in (1, 7, 10):
        ts(T.w[0:8, :, j], YB, Q16, None, A.is_equal, deps=[io_y])
    ts(T.w[0:8, :, 3], YB, Q32, 0.5, A.is_equal, A.mult)
    ts(T.w[0:8, :, 4], YB, Q32, -1.0, A.is_gt, A.mult)
    ts(T.w[0:8, :, 5], YB, Q16, -1.0, A.is_equal, A.mult)
    e1 = ts(T.e1[0:8, :], YB, 16.0, Q16, A.add, A.is_equal)
    ts(T.g2[:], T.Y[:], -32.0, P32, A.add, A.is_ge)
    for h in range(2):
        ts(T.sp[:, h, :], T.Y[:], 16.0 * h, P, A.add, A.is_equal)
        su = ts(T.su[:, h, :], T.Y[:], 16.0 * h, P, A.add, A.is_gt)
    tt(T.w[0:8, :, 2], T.w[0:8, :, 4], T.w[0:8, :, 3], A.subtract, [e1])
    tt(T.w[0:8, :, 11], T.e1[0:8, :], T.w[0:8, :, 10], A.subtract)
    for h in range(2):
        st = tt(T.st[:, h, :], T.su[:, h, :], T.g2[:], A.subtract, [su])

    for t in range(4):
        tI = ts(T.tI[:, :, t, :], T.nC[:], T.psA[:, 2 * t:2 * t + 1], T.psA[:, 2 * t + 1:2 * t + 2], A.mult, A.add,
                [mab, nc1])
    uI = ts(T.uI[:], T.tI[:], 2, 1023, sr, an, [tI])
    uF = cp(T.uF[:], T.uI[:], [uI])

    cv = cp(T.cpad[0:8, 96:128], T.c8[0:8, :], [("d_c8", 16)])
    for b in range(4):
        m1 = mm(T.psB[:, 0:12], T.cpad[0:8, 96 - 32 * b:224 - 32 * b], T.w[0:8, b, :], b == 0, b == 3, [cv, st])
    bp = ts(T.bp[:], T.X[:, 0:32], T.colf[:, 4:5], T.colf[:, 5:6], A.subtract, A.is_equal)
    ev = cp(T.ev[:], T.psB[:, 0:12], [m1])
    bm = ts(T.bm[:], T.bp[:], -1.0, None, A.mult, deps=[bp])
    for h in range(2):
        mm(T.psC[:, 6 * h:6 * h + 6], T.sp[:, h, :], T.ev[:, 0:6], True, False, [ev])
        m2 = mm(T.psC[:, 6 * h:6 * h + 6], T.st[:, h, :], T.ev[:, 6:12], False, True)
    zc = ms(T.xs[:, ZERO:ZERO + 16], 0.0)
    tb = tt(T.tb[:, :, 0:6], T.psC[:, 0:12], T.kc[:, :, 0:6], A.add, [m2, kc])
    idxu = [cp(T.idxu[:, 0, :], T.idxi[:, 0, :], [("d_i0", 32)])]

    for h in range(2):
        col = [T.tb[:, h, j:j + 1] for j in range(6)]
        mf = act(T.mf[:, h::2], T.uF[:, h::2], F.Identity, [tb, uF], bias=col[4], scale=col[0])
        ad = act(T.ad[:, h::2], T.uF[:, h::2], F.Abs, bias=col[2], scale=col[0])
        ts(T.psD[:, h:256:2], T.mf[:, h::2], col[1], col[5], A.is_ge, A.mult, [mf, tb])
        pen = ts(T.psD[:, 256 + h::2], T.ad[:, h::2], col[3], BIG, A.is_gt, A.mult, [ad])
    s1 = tt(T.s1[:], T.mf[:], T.psD[:, 0:256], A.add, [pen])
    s2 = tt(T.s2[:], T.s1[:], T.psD[:, 256:512], A.add, [s1])
    offs = ts(T.offs[:], T.s2[:], float(ZERO), None, A.min, deps=[s2])

    done = []
    for blk, cut, sem in ((0, 80, ("d_x0", 32)), (1, 64, ("d_x1", 64))):
        if blk == 1:
            idxu.append(cp(T.idxu[:, 1, :], T.idxi[:, 1, :], [("d_i1", 32)]))
        for q, c0, c1 in (("s", 0, cut), ("v", cut, 128)):
            o = 2048 * blk
            done.append(gather(q, T.xs[:, o + 16 * c0:o + 16 * c1], T.x0[:, blk, :], T.idxu[:, blk, c0:c1],
                               [idxu[blk], sem]))

    ready = [done[-1], done[-2], offs]
    z3 = []
    last = []
    for ch in range(8):
        got = gather("vs"[ch % 2], T.gt[:, 512 * ch:512 * ch + 512], T.xs[:, :], T.offs[:, 32 * ch:32 * ch + 32], ready)
        bank = (T.psE, T.psF)[ch // 4]
        for j in range(2 * ch, 2 * ch + 2):
            out = bank[:, 32 * (j % 8):32 * (j % 8) + 32]
            mm(out, T.gt[:, 256 * j:256 * j + 128], T.bp[:], True, False, [got, bm])
            m = mm(out, T.gt[:, 256 * j + 128:256 * j + 256], T.bm[:], False, True)
        if ch % 4 == 3:
            last.append(m)
    for h, (bank, up) in enumerate(((T.psE, T.psG), (T.psF, T.psH))):
        act(T.zl[:, h, :], bank[:, 0:128], F.Abs, [last[h]])
        zu = act(up[:, 0:128], bank[:, 128:256], F.Abs)
        z1 = tt(T.z1[:, h, :], T.zl[:, h, :], up[:, 0:128], A.add, [zu])
        z2 = tt(T.z2[:, h, :], T.z1[:, h, 0:64], T.z1[:, h, 64:128], A.add, [z1])
        z3 = tt(T.z3[:, h, :], T.z2[:, h, 0:32], T.z2[:, h, 32:64], A.add, [z2])
    z4 = tt(T.z4[:], T.z3[:, 0, :], T.z3[:, 1, :], A.add, [z3])
    yt = op("v", lambda: g.vector.transpose(T.yt[:], T.z4[:]), [z4])

    def place(r):
        return 2 * (r % 4) + r // 4

    dma("y", T.dz[:], T.yt[:], "d_z", [yt])
    dma("s", T.ly[rank], T.yt[16 * place(rank):16 * place(rank) + 16, :], "d_oz", [yt])
    send([(k, "res_in") for k in everyone], lambda k: T.dz[place(rank ^ k)], lambda k: T.ly[rank], [("d_z", 16)])
    dma("y", T.y[:], T.ly[:], "d_y", [("res_in", NE), ("d_oz", 16)])

    count = {q: 0 for q in QS}
    seen = {q: {} for q in Q}
    for o in ops:
        q = o["q"]
        want = {}
        for d in o["deps"]:
            name, val = ("q" + d["q"], d["at"]) if isinstance(d, dict) else d
            want[name] = max(want.get(name, 0), val)
        for name, val in want.items():
            if seen[q].get(name, 0) < val:
                Q[q].wait_ge(S[name], val)
                seen[q][name] = val
        ins = o["fn"]()
        if o["dma"] is not None:
            ins.then_inc(S[o["dma"]], 16)
        elif o["need"]:
            count[q] += 1
            o["at"] = count[q]
            ins.then_inc(QS[q], 1)
    g.wait_ge(S.sent, sent[0])
    g.sync.wait_ge(S.d_y, 16)
